import numpy as np
import ml_dtypes


def mxq(x, axis, fmt="e4m3"):
    dtype, down = {"e4m3": (ml_dtypes.float8_e4m3fn, 7), "e5m2": (ml_dtypes.float8_e5m2, 14)}[fmt]
    v = np.moveaxis(np.asarray(x, np.float32).astype(ml_dtypes.bfloat16).astype(np.float64), axis, -1)
    blocks = v.reshape(v.shape[:-1] + (-1, 32))
    amax = np.abs(blocks).max(-1, keepdims=True)
    byte = np.maximum(np.where(amax > 0, np.frexp(amax)[1] - 1 + 127, 0) - down, 1)
    scale = np.exp2(byte - 127.0)
    codes = (blocks / scale).astype(np.float32).astype(dtype).astype(np.float64)
    return np.moveaxis((codes * scale).reshape(v.shape), -1, axis)


WIDE = False


def mx_kscale(k):
    if not WIDE:
        return np.ones(k)
    levels = np.array([10, -10, 5, -5, 0])
    if k % 512:
        return np.exp2(np.random.permutation(np.resize(levels, k // 32))).repeat(32)
    a = np.empty((k // 512, 16))
    for p in range(k // 512):
        a[p, :8] = np.random.permutation(np.resize(levels, 8))
        for g in range(8):
            far = levels[np.abs(levels - a[p, g]) >= 10]
            a[p, g + 8] = far[np.random.randint(len(far))]
    return np.exp2(a.ravel()).repeat(32)


def f64(x):
    return np.asarray(x).astype(np.float64)


def striped(idx):
    return np.tile(np.asarray(idx).reshape(-1, 16).T, (8, 1)).astype(np.uint16)


def unstriped(offs):
    return offs[:16].T.reshape(-1).astype(np.int64)

def rot(x):
    y = x.reshape(x.shape[0], -1, 2, x.shape[2])
    return np.stack([-y[:, :, 1], y[:, :, 0]], axis=2).reshape(x.shape)


B, N, T, D, NQ = 1, 512, 2048, 512, 256


def setup_inputs():
    n = np.random.standard_normal
    idx = np.random.permutation(T)[:B * N]
    idx2 = np.random.permutation(1024)[:B * N]
    s = mx_kscale(D)[:, None]
    return {
        "qT": (n((B, D, NQ)) * s * (1.00 / np.sqrt(D))).astype(np.float32),
        "kT": (np.clip(np.round(n((D, T)) * 16), -64, 64) / 16 / s).astype(np.float32),
        "cT": (np.repeat(np.round(np.cos(np.arange(D // 2)[:, None] * 0.11 + np.arange(1024)[None] * 0.37) * 64) / 64, 2, axis=0)).astype(np.float32),
        "wT": (np.repeat(np.round(np.sin(np.arange(D // 2)[:, None] * 0.11 + np.arange(1024)[None] * 0.37) * 64) / 64, 2, axis=0)).astype(np.float32),
        "offs": striped(idx),
        "offs2": striped(idx2),
    }


def reference(qT, kT, cT, wT, offs, offs2):
    idx = unstriped(offs)
    idx2 = unstriped(offs2)
    pick = lambda x, which: x[:, which].reshape(x.shape[0], B, -1).transpose(1, 0, 2)
    kg = pick(f64(kT), idx)
    cg = pick(f64(cT), idx2)
    wg = pick(f64(wT), idx2)
    ug = mxq(kg * cg + rot(kg) * wg, 1, "e4m3")
    qq = mxq(f64(qT), 1, "e4m3")
    a = qq.transpose(0, 2, 1) @ ug
    return a

@@ -1,0 +1,127 @@
+from contextlib import ExitStack
+
+import concourse.mybir as mybir
+
+D, T, POS, N, NQ = 512, 2048, 1024, 512, 256
+FLOPS = 2 * D * N * NQ
+
+F32 = mybir.dt.float32
+BF16 = mybir.dt.bfloat16
+U32 = mybir.dt.uint32
+U16 = mybir.dt.uint16
+U8 = mybir.dt.uint8
+FP8X4 = mybir.dt.float8_e4m3fn_x4
+MULT = mybir.AluOpType.mult
+ADD = mybir.AluOpType.add
+COPY = mybir.ActivationFunctionType.Copy
+
+P = 128
+PACK = 4
+HALF = N // 2
+
+
+def tile_attend_pre_rope_f_topk_kernel(tc, qT, kT, cT, wT, offs, offs2, out):
+    nc = tc.nc
+    with ExitStack() as ctx:
+        pool = ctx.enter_context(tc.tile_pool(name="held", bufs=1))
+        psum = ctx.enter_context(tc.psum_pool(name="psum", bufs=1))
+
+        tok = pool.tile([P, N // 16], U16, name="tok")
+        pos = pool.tile([P, N // 16], U16, name="pos")
+        kp = [pool.tile([P, T], F32, name="kp%d" % t) for t in range(PACK)]
+        cp = [pool.tile([P, POS], F32, name="cp%d" % t) for t in range(PACK)]
+        wp = [pool.tile([P, POS], F32, name="wp%d" % t) for t in range(PACK)]
+        q_raw = pool.tile([P, PACK, NQ], F32, name="q_raw")
+        kv = kT.rearrange("(p t) n -> p t n", t=PACK)
+        cv = cT.rearrange("(p t) n -> p t n", t=PACK)
+        wv = wT.rearrange("(p t) n -> p t n", t=PACK)
+
+        nc.sync.dma_start(out=kp[0][:], in_=kv[:, 0, :])
+        nc.sync.dma_start(tok[:], offs)
+        nc.sync.dma_start(pos[:], offs2)
+        for t in range(PACK):
+            if t > 0:
+                nc.sync.dma_start(out=kp[t][:], in_=kv[:, t, :])
+            nc.sync.dma_start(out=cp[t][:], in_=cv[:, t, :])
+            nc.sync.dma_start(out=wp[t ^ 1][:], in_=wv[:, t ^ 1, :])
+        nc.sync.dma_start(out=q_raw[:], in_=qT[0].rearrange("(p t) n -> p t n", t=PACK))
+
+        kg = [pool.tile([P, N], F32, name="kg%d" % t) for t in range(PACK)]
+        kneg = [pool.tile([P, N], F32, name="kneg%d" % h) for h in range(2)]
+        kc = pool.tile([P, PACK, N], F32, name="kc")
+        kw = pool.tile([P, PACK, N], F32, name="kw")
+        u = pool.tile([P, N, PACK], BF16, name="u", align_bytes=64)
+        u_codes = pool.tile([P, N], U32, name="u_codes", align_bytes=64)
+        u_scales = pool.tile([P, N], U8, name="u_scales", align_bytes=64)
+        qb = pool.tile([P, NQ, PACK], BF16, name="qb", align_bytes=64)
+        q_codes = pool.tile([P, NQ], U32, name="q_codes", align_bytes=64)
+        q_scales = pool.tile([P, NQ], U8, name="q_scales", align_bytes=64)
+        res = pool.tile([P, 2, 2, HALF], F32, name="res")
+        acc = [[psum.tile([P, HALF], F32, name="acc%d%d" % (h, m)) for m in range(2)] for h in range(2)]
+
+        def rotated(t):
+            return kneg[t // 2] if t % 2 else kg[t]
+
+        def sine_product(t, lo, hi):
+            nc.vector.tensor_tensor(kw[:, t ^ 1, lo:hi], wp[t ^ 1][:].indirect(pos[:, lo // 16 : hi // 16]), rotated(t)[:, lo:hi], MULT)
+
+        def add_half(h):
+            cols = slice(h * HALF, (h + 1) * HALF)
+            nc.vector.tensor_tensor(
+                u[:, cols, :].rearrange("p (c i) t -> p c t i", i=2),
+                kc[:, :, cols].rearrange("p t (c i) -> p c t i", i=2),
+                kw[:, :, cols].rearrange("p t (c i) -> p c t i", i=2),
+                ADD,
+            )
+
+        def quantize_half(h):
+            cols = slice(h * HALF, (h + 1) * HALF)
+            nc.vector.quantize_mx(
+                out=u_codes[:, cols].bitcast(FP8X4),
+                scales=u_scales[:, cols],
+                in_=u[:, cols, :].rearrange("p n t -> p (n t)"),
+            )
+
+        def scores(h):
+            cols = slice(h * HALF, (h + 1) * HALF)
+            for m in range(2):
+                rows = slice(m * P, (m + 1) * P)
+                nc.tensor.matmul_mx(
+                    out=acc[h][m][:],
+                    lhsT=q_codes[:, rows].bitcast(FP8X4),
+                    lhsT_scale=q_scales[:, rows],
+                    rhs=u_codes[:, cols].bitcast(FP8X4),
+                    rhs_scale=u_scales[:, cols],
+                    start=True,
+                    stop=True,
+                )
+
+        for t in range(PACK):
+            nc.vector.tensor_copy(kg[t][:], kp[t][:].indirect(tok[:]))
+            if t % 2:
+                nc.scalar.activation(kneg[t // 2][:], kg[t][:], COPY, scale=-1.0)
+            nc.vector.tensor_tensor(kc[:, t, :], cp[t][:].indirect(pos[:]), kg[t][:], MULT)
+            if t < PACK - 1:
+                sine_product(t, 0, N)
+
+        nc.scalar.copy(
+            qb[:].rearrange("p (c i) t -> p c t i", i=2),
+            q_raw[:].rearrange("p t (c i) -> p c t i", i=2),
+        )
+
+        sine_product(PACK - 1, 0, HALF)
+        sine_product(PACK - 1, HALF, N)
+        add_half(0)
+        nc.vector.quantize_mx(out=q_codes[:].bitcast(FP8X4), scales=q_scales[:], in_=qb[:].rearrange("p n t -> p (n t)"))
+        quantize_half(0)
+        add_half(1)
+        scores(0)
+        for m in range(2):
+            nc.scalar.copy(res[:, 0, m, :], acc[0][m][:])
+        nc.sync.dma_start(out=out[0].rearrange("(m p) n -> p m n", p=P)[:, :, 0:HALF], in_=res[:, 0, :, :])
+        quantize_half(1)
+        scores(1)
+        nc.scalar.copy(res[:, 1, 0, :], acc[1][0][:])
+        nc.scalar.dma_start(out=out[0, 0:P, HALF:N], in_=res[:, 1, 0, :])
+        nc.vector.tensor_copy(res[:, 1, 1, :], acc[1][1][:])
+        nc.sync.dma_start(out=out[0, P:NQ, HALF:N], in_=res[:, 1, 1, :])

@@ -4,6 +4,7 @@ import concourse.mybir as mybir
 
 D, T, POS, N, NQ = 512, 2048, 1024, 512, 256
 FLOPS = 2 * D * N * NQ
+BYTES = 4 * (D * NQ + D * T + D * POS + NQ * N) + 2 * 2 * 128 * (N // 16)
 
 F32 = mybir.dt.float32
 BF16 = mybir.dt.bfloat16
@@ -17,7 +18,7 @@ COPY = mybir.ActivationFunctionType.Copy
 
 P = 128
 PACK = 4
-HALF = N // 2
+CHUNKS = ((0, 256), (256, 384), (384, 512))
 
 
 def tile_attend_pre_rope_f_topk_kernel(tc, qT, kT, cT, wT, offs, offs2, out):
@@ -29,25 +30,27 @@ def tile_attend_pre_rope_f_topk_kernel(tc, qT, kT, cT, wT, offs, offs2, out):
         tok = pool.tile([P, N // 16], U16, name="tok")
         pos = pool.tile([P, N // 16], U16, name="pos")
         kp = [pool.tile([P, T], F32, name="kp%d" % t) for t in range(PACK)]
-        cp = [pool.tile([P, POS], F32, name="cp%d" % t) for t in range(PACK)]
-        wp = [pool.tile([P, POS], F32, name="wp%d" % t) for t in range(PACK)]
+        cp = [pool.tile([P, POS], F32, name="cp%d" % h) for h in range(2)]
+        wp = [pool.tile([P, POS], F32, name="wp%d" % h) for h in range(2)]
         q_raw = pool.tile([P, PACK, NQ], F32, name="q_raw")
         kv = kT.rearrange("(p t) n -> p t n", t=PACK)
         cv = cT.rearrange("(p t) n -> p t n", t=PACK)
         wv = wT.rearrange("(p t) n -> p t n", t=PACK)
 
-        nc.sync.dma_start(out=kp[0][:], in_=kv[:, 0, :])
-        nc.sync.dma_start(tok[:], offs)
-        nc.sync.dma_start(pos[:], offs2)
-        for t in range(PACK):
-            if t > 0:
+        for h in range(2):
+            nc.sync.dma_start(out=cp[h][:], in_=cv[:, 2 * h, :])
+            if h == 0:
+                nc.sync.dma_start(pos[:], offs2)
+            nc.sync.dma_start(out=wp[h][:], in_=wv[:, 2 * h, :])
+            if h == 0:
+                nc.sync.dma_start(tok[:], offs)
+            for t in (2 * h, 2 * h + 1):
                 nc.sync.dma_start(out=kp[t][:], in_=kv[:, t, :])
-            nc.sync.dma_start(out=cp[t][:], in_=cv[:, t, :])
-            nc.sync.dma_start(out=wp[t ^ 1][:], in_=wv[:, t ^ 1, :])
         nc.sync.dma_start(out=q_raw[:], in_=qT[0].rearrange("(p t) n -> p t n", t=PACK))
 
-        kg = [pool.tile([P, N], F32, name="kg%d" % t) for t in range(PACK)]
-        kneg = [pool.tile([P, N], F32, name="kneg%d" % h) for h in range(2)]
+        cg = [pool.tile([P, N], F32, name="cg%d" % h) for h in range(2)]
+        wg = [pool.tile([P, N], F32, name="wg%d" % h) for h in range(2)]
+        wneg = [pool.tile([P, N], F32, name="wneg%d" % h) for h in range(2)]
         kc = pool.tile([P, PACK, N], F32, name="kc")
         kw = pool.tile([P, PACK, N], F32, name="kw")
         u = pool.tile([P, N, PACK], BF16, name="u", align_bytes=64)
@@ -56,17 +59,19 @@ def tile_attend_pre_rope_f_topk_kernel(tc, qT, kT, cT, wT, offs, offs2, out):
         qb = pool.tile([P, NQ, PACK], BF16, name="qb", align_bytes=64)
         q_codes = pool.tile([P, NQ], U32, name="q_codes", align_bytes=64)
         q_scales = pool.tile([P, NQ], U8, name="q_scales", align_bytes=64)
-        res = pool.tile([P, 2, 2, HALF], F32, name="res")
-        acc = [[psum.tile([P, HALF], F32, name="acc%d%d" % (h, m)) for m in range(2)] for h in range(2)]
+        res = [pool.tile([P, 2, hi - lo], F32, name="res%d" % lo) for lo, hi in CHUNKS]
+        acc = [psum.tile([P, 2, hi - lo], F32, name="acc%d" % lo) for lo, hi in CHUNKS]
+        out_v = out[0].rearrange("(m p) n -> p m n", p=P)
 
-        def rotated(t):
-            return kneg[t // 2] if t % 2 else kg[t]
+        def cos_product(t, lo, hi):
+            nc.vector.tensor_tensor(kc[:, t, lo:hi], kp[t][:].indirect(tok[:, lo // 16 : hi // 16]), cg[t // 2][:, lo:hi], MULT)
 
-        def sine_product(t, lo, hi):
-            nc.vector.tensor_tensor(kw[:, t ^ 1, lo:hi], wp[t ^ 1][:].indirect(pos[:, lo // 16 : hi // 16]), rotated(t)[:, lo:hi], MULT)
+        def sin_product(t, lo, hi):
+            w = wneg[t // 2] if t % 2 else wg[t // 2]
+            nc.vector.tensor_tensor(kw[:, t ^ 1, lo:hi], kp[t][:].indirect(tok[:, lo // 16 : hi // 16]), w[:, lo:hi], MULT)
 
-        def add_half(h):
-            cols = slice(h * HALF, (h + 1) * HALF)
+        def add(j):
+            cols = slice(*CHUNKS[j])
             nc.vector.tensor_tensor(
                 u[:, cols, :].rearrange("p (c i) t -> p c t i", i=2),
                 kc[:, :, cols].rearrange("p t (c i) -> p c t i", i=2),
@@ -74,20 +79,20 @@ def tile_attend_pre_rope_f_topk_kernel(tc, qT, kT, cT, wT, offs, offs2, out):
                 ADD,
             )
 
-        def quantize_half(h):
-            cols = slice(h * HALF, (h + 1) * HALF)
+        def quantize(j):
+            cols = slice(*CHUNKS[j])
             nc.vector.quantize_mx(
                 out=u_codes[:, cols].bitcast(FP8X4),
                 scales=u_scales[:, cols],
                 in_=u[:, cols, :].rearrange("p n t -> p (n t)"),
             )
 
-        def scores(h):
-            cols = slice(h * HALF, (h + 1) * HALF)
+        def scores(j):
+            cols = slice(*CHUNKS[j])
             for m in range(2):
                 rows = slice(m * P, (m + 1) * P)
                 nc.tensor.matmul_mx(
-                    out=acc[h][m][:],
+                    out=acc[j][:, m, :],
                     lhsT=q_codes[:, rows].bitcast(FP8X4),
                     lhsT_scale=q_scales[:, rows],
                     rhs=u_codes[:, cols].bitcast(FP8X4),
@@ -96,32 +101,38 @@ def tile_attend_pre_rope_f_topk_kernel(tc, qT, kT, cT, wT, offs, offs2, out):
                     stop=True,
                 )
 
-        for t in range(PACK):
-            nc.vector.tensor_copy(kg[t][:], kp[t][:].indirect(tok[:]))
-            if t % 2:
-                nc.scalar.activation(kneg[t // 2][:], kg[t][:], COPY, scale=-1.0)
-            nc.vector.tensor_tensor(kc[:, t, :], cp[t][:].indirect(pos[:]), kg[t][:], MULT)
-            if t < PACK - 1:
-                sine_product(t, 0, N)
+        for h in range(2):
+            nc.vector.tensor_copy(cg[h][:], cp[h][:].indirect(pos[:]))
+            nc.vector.tensor_copy(wg[h][:], wp[h][:].indirect(pos[:]))
+            nc.scalar.activation(wneg[h][:], wg[h][:], COPY, scale=-1.0)
+            for t in (2 * h, 2 * h + 1):
+                if t < PACK - 1:
+                    cos_product(t, 0, N)
+                    sin_product(t, 0, N)
 
         nc.scalar.copy(
             qb[:].rearrange("p (c i) t -> p c t i", i=2),
             q_raw[:].rearrange("p t (c i) -> p c t i", i=2),
         )
 
-        sine_product(PACK - 1, 0, HALF)
-        sine_product(PACK - 1, HALF, N)
-        add_half(0)
+        last = PACK - 1
+        cos_product(last, 0, 256)
+        sin_product(last, 0, 256)
+        cos_product(last, 256, N)
+        add(0)
+        sin_product(last, 256, N)
         nc.vector.quantize_mx(out=q_codes[:].bitcast(FP8X4), scales=q_scales[:], in_=qb[:].rearrange("p n t -> p (n t)"))
-        quantize_half(0)
-        add_half(1)
+        quantize(0)
         scores(0)
-        for m in range(2):
-            nc.scalar.copy(res[:, 0, m, :], acc[0][m][:])
-        nc.sync.dma_start(out=out[0].rearrange("(m p) n -> p m n", p=P)[:, :, 0:HALF], in_=res[:, 0, :, :])
-        quantize_half(1)
+        nc.scalar.copy(res[0][:], acc[0][:])
+        nc.sync.dma_start(out=out_v[:, :, 0:256], in_=res[0][:])
+        add(1)
+        add(2)
+        quantize(1)
+        quantize(2)
         scores(1)
-        nc.scalar.copy(res[:, 1, 0, :], acc[1][0][:])
-        nc.scalar.dma_start(out=out[0, 0:P, HALF:N], in_=res[:, 1, 0, :])
-        nc.vector.tensor_copy(res[:, 1, 1, :], acc[1][1][:])
-        nc.sync.dma_start(out=out[0, P:NQ, HALF:N], in_=res[:, 1, 1, :])
+        scores(2)
+        nc.scalar.copy(res[1][:], acc[1][:])
+        nc.scalar.dma_start(out=out_v[:, :, 256:384], in_=res[1][:])
+        nc.vector.tensor_copy(res[2][:], acc[2][:])
+        nc.sync.dma_start(out=out_v[:, :, 384:512], in_=res[2][:])

@@ -1,6 +1,7 @@
 from contextlib import ExitStack
 
 import concourse.mybir as mybir
+from concourse.masks import make_identity
 
 D, T, POS, N, NQ = 512, 2048, 1024, 512, 256
 FLOPS = 2 * D * N * NQ
@@ -19,6 +20,7 @@ COPY = mybir.ActivationFunctionType.Copy
 P = 128
 PACK = 4
 CHUNKS = ((0, 256), (256, 384), (384, 512))
+EARLY = 384
 
 
 def tile_attend_pre_rope_f_topk_kernel(tc, qT, kT, cT, wT, offs, offs2, out):
@@ -37,30 +39,41 @@ def tile_attend_pre_rope_f_topk_kernel(tc, qT, kT, cT, wT, offs, offs2, out):
         cv = cT.rearrange("(p t) n -> p t n", t=PACK)
         wv = wT.rearrange("(p t) n -> p t n", t=PACK)
 
-        for h in range(2):
-            nc.sync.dma_start(out=cp[h][:], in_=cv[:, 2 * h, :])
-            if h == 0:
-                nc.sync.dma_start(pos[:], offs2)
-            nc.sync.dma_start(out=wp[h][:], in_=wv[:, 2 * h, :])
-            if h == 0:
-                nc.sync.dma_start(tok[:], offs)
-            for t in (2 * h, 2 * h + 1):
-                nc.sync.dma_start(out=kp[t][:], in_=kv[:, t, :])
+        nc.sync.dma_start(out=wp[0][:], in_=wv[:, 0, :])
+        nc.sync.dma_start(pos[:], offs2)
+        nc.sync.dma_start(out=cp[0][:], in_=cv[:, 0, :])
+        nc.sync.dma_start(out=wp[1][:], in_=wv[:, 2, :])
+        nc.sync.dma_start(out=cp[1][:], in_=cv[:, 2, :])
+        nc.sync.dma_start(tok[:], offs)
+        for t in range(PACK):
+            nc.sync.dma_start(out=kp[t][:], in_=kv[:, t, :])
         nc.sync.dma_start(out=q_raw[:], in_=qT[0].rearrange("(p t) n -> p t n", t=PACK))
+
+        ident = pool.tile([P, P], F32, name="ident")
+        make_identity(nc, ident[:])
 
         cg = [pool.tile([P, N], F32, name="cg%d" % h) for h in range(2)]
         wg = [pool.tile([P, N], F32, name="wg%d" % h) for h in range(2)]
         wneg = [pool.tile([P, N], F32, name="wneg%d" % h) for h in range(2)]
         kc = pool.tile([P, PACK, N], F32, name="kc")
         kw = pool.tile([P, PACK, N], F32, name="kw")
+        turned = pool.tile([P, 2, EARLY], F32, name="turned")
+        pairs = pool.tile([P, 2, EARLY, 2], BF16, name="pairs", align_bytes=64)
         u = pool.tile([P, N, PACK], BF16, name="u", align_bytes=64)
         u_codes = pool.tile([P, N], U32, name="u_codes", align_bytes=64)
         u_scales = pool.tile([P, N], U8, name="u_scales", align_bytes=64)
         qb = pool.tile([P, NQ, PACK], BF16, name="qb", align_bytes=64)
         q_codes = pool.tile([P, NQ], U32, name="q_codes", align_bytes=64)
         q_scales = pool.tile([P, NQ], U8, name="q_scales", align_bytes=64)
-        res = [pool.tile([P, 2, hi - lo], F32, name="res%d" % lo) for lo, hi in CHUNKS]
-        acc = [psum.tile([P, 2, hi - lo], F32, name="acc%d" % lo) for lo, hi in CHUNKS]
+        res0 = pool.tile([P, 2, 256], F32, name="res0")
+        res1 = pool.tile([P, 2, P], F32, name="res1")
+        res2 = pool.tile([P, 2, P], F32, name="res2")
+        sums = [psum.tile([P, EARLY], F32, name="sums%d" % t, tag="bank%d" % t) for t in range(2)]
+        acc0 = psum.tile([P, 2, 256], F32, name="acc0")
+        acc2 = [psum.tile([P, P], F32, name="acc2%d" % m) for m in range(2)]
+        u_words = u[:].rearrange("p n t -> p (n t)").bitcast(F32)
+        pair_words = pairs[:].rearrange("p h n e -> p h (n e)").bitcast(F32)
+        back = [psum.tile([P, 2, hi - lo], F32, name="back%d" % lo) for lo, hi in CHUNKS[:2]]
         out_v = out[0].rearrange("(m p) n -> p m n", p=P)
 
         def cos_product(t, lo, hi):
@@ -69,6 +82,36 @@ def tile_attend_pre_rope_f_topk_kernel(tc, qT, kT, cT, wT, offs, offs2, out):
         def sin_product(t, lo, hi):
             w = wneg[t // 2] if t % 2 else wg[t // 2]
             nc.vector.tensor_tensor(kw[:, t ^ 1, lo:hi], kp[t][:].indirect(tok[:, lo // 16 : hi // 16]), w[:, lo:hi], MULT)
+
+        def early_sum(t):
+            for b in range(EARLY // P):
+                cols = slice(b * P, (b + 1) * P)
+                nc.tensor.matmul(sums[t][:, cols], kc[:, t, cols], ident[:], start=True, stop=False, is_transpose=True)
+                nc.tensor.matmul(sums[t][:, cols], kw[:, t, cols], ident[:], start=False, stop=True, is_transpose=True)
+            nc.scalar.copy(turned[:, t, :], sums[t][:])
+
+        def early_back(j):
+            lo, hi = CHUNKS[j]
+            for t in (1, 0):
+                for c in range(lo, hi, P):
+                    nc.tensor.transpose(back[j][:, t, c - lo : c - lo + P], turned[:, t, c : c + P], ident[:])
+            nc.scalar.copy(
+                pairs[:, 0, lo:hi, :].rearrange("p (c i) e -> p c e i", i=4),
+                back[j][:].rearrange("p e (c i) -> p c e i", i=4),
+            )
+
+        def add_late_pair(j):
+            cols = slice(*CHUNKS[j])
+            nc.vector.tensor_tensor(
+                pairs[:, 1, cols, :].rearrange("p (c i) e -> p c e i", i=4),
+                kc[:, 2:4, cols].rearrange("p e (c i) -> p c e i", i=4),
+                kw[:, 2:4, cols].rearrange("p e (c i) -> p c e i", i=4),
+                ADD,
+            )
+            nc.scalar.copy(
+                u_words[:, 2 * cols.start : 2 * cols.stop].rearrange("p (n h) -> p n h", h=2),
+                pair_words[:, :, cols].rearrange("p h n -> p n h"),
+            )
 
         def add(j):
             cols = slice(*CHUNKS[j])
@@ -87,12 +130,12 @@ def tile_attend_pre_rope_f_topk_kernel(tc, qT, kT, cT, wT, offs, offs2, out):
                 in_=u[:, cols, :].rearrange("p n t -> p (n t)"),
             )
 
-        def scores(j):
+        def scores(j, accs):
             cols = slice(*CHUNKS[j])
             for m in range(2):
                 rows = slice(m * P, (m + 1) * P)
                 nc.tensor.matmul_mx(
-                    out=acc[j][:, m, :],
+                    out=accs[m],
                     lhsT=q_codes[:, rows].bitcast(FP8X4),
                     lhsT_scale=q_scales[:, rows],
                     rhs=u_codes[:, cols].bitcast(FP8X4),
@@ -102,13 +145,18 @@ def tile_attend_pre_rope_f_topk_kernel(tc, qT, kT, cT, wT, offs, offs2, out):
                 )
 
         for h in range(2):
-            nc.vector.tensor_copy(cg[h][:], cp[h][:].indirect(pos[:]))
             nc.vector.tensor_copy(wg[h][:], wp[h][:].indirect(pos[:]))
             nc.scalar.activation(wneg[h][:], wg[h][:], COPY, scale=-1.0)
-            for t in (2 * h, 2 * h + 1):
-                if t < PACK - 1:
-                    cos_product(t, 0, N)
-                    sin_product(t, 0, N)
+            nc.vector.tensor_copy(cg[h][:], cp[h][:].indirect(pos[:]))
+        for t in range(PACK - 1):
+            cos_product(t, 0, N)
+            if t == 1:
+                early_sum(1)
+            sin_product(t, 0, N)
+            if t == 1:
+                early_sum(0)
+                early_back(0)
+                early_back(1)
 
         nc.scalar.copy(
             qb[:].rearrange("p (c i) t -> p c t i", i=2),
@@ -119,20 +167,23 @@ def tile_attend_pre_rope_f_topk_kernel(tc, qT, kT, cT, wT, offs, offs2, out):
         cos_product(last, 0, 256)
         sin_product(last, 0, 256)
         cos_product(last, 256, N)
-        add(0)
+        add_late_pair(0)
         sin_product(last, 256, N)
         nc.vector.quantize_mx(out=q_codes[:].bitcast(FP8X4), scales=q_scales[:], in_=qb[:].rearrange("p n t -> p (n t)"))
         quantize(0)
-        scores(0)
-        nc.scalar.copy(res[0][:], acc[0][:])
-        nc.sync.dma_start(out=out_v[:, :, 0:256], in_=res[0][:])
-        add(1)
+        add_late_pair(1)
+        scores(0, [acc0[:, 0, :], acc0[:, 1, :]])
         add(2)
+        nc.scalar.copy(res0[:], acc0[:])
+        nc.sync.dma_start(out=out_v[:, :, 0:256], in_=res0[:])
         quantize(1)
         quantize(2)
-        scores(1)
-        scores(2)
-        nc.scalar.copy(res[1][:], acc[1][:])
-        nc.scalar.dma_start(out=out_v[:, :, 256:384], in_=res[1][:])
-        nc.vector.tensor_copy(res[2][:], acc[2][:])
-        nc.sync.dma_start(out=out_v[:, :, 384:512], in_=res[2][:])
+        acc1 = [psum.tile([P, P], F32, name="acc1%d" % m, tag="bank%d" % m) for m in range(2)]
+        scores(1, [acc1[0][:], acc1[1][:]])
+        scores(2, [acc2[0][:], acc2[1][:]])
+        nc.scalar.copy(res1[:, 0, :], acc1[0][:])
+        nc.vector.tensor_copy(res1[:, 1, :], acc1[1][:])
+        nc.sync.dma_start(out=out_v[:, :, 256:384], in_=res1[:])
+        nc.scalar.copy(res2[:, 0, :], acc2[0][:])
+        nc.vector.tensor_copy(res2[:, 1, :], acc2[1][:])
+        nc.sync.dma_start(out=out_v[:, :, 384:N], in_=res2[:])

@@ -57,7 +57,7 @@ def tile_attend_pre_rope_f_topk_kernel(tc, qT, kT, cT, wT, offs, offs2, out):
         wneg = [pool.tile([P, N], F32, name="wneg%d" % h) for h in range(2)]
         kc = pool.tile([P, PACK, N], F32, name="kc")
         kw = pool.tile([P, PACK, N], F32, name="kw")
-        turned = pool.tile([P, 2, EARLY], F32, name="turned")
+        turned = pool.tile([P, EARLY, 2], BF16, name="turned", align_bytes=64)
         pairs = pool.tile([P, 2, EARLY, 2], BF16, name="pairs", align_bytes=64)
         u = pool.tile([P, N, PACK], BF16, name="u", align_bytes=64)
         u_codes = pool.tile([P, N], U32, name="u_codes", align_bytes=64)
@@ -68,12 +68,12 @@ def tile_attend_pre_rope_f_topk_kernel(tc, qT, kT, cT, wT, offs, offs2, out):
         res0 = pool.tile([P, 2, 256], F32, name="res0")
         res1 = pool.tile([P, 2, P], F32, name="res1")
         res2 = pool.tile([P, 2, P], F32, name="res2")
-        sums = [psum.tile([P, EARLY], F32, name="sums%d" % t, tag="bank%d" % t) for t in range(2)]
-        acc0 = psum.tile([P, 2, 256], F32, name="acc0")
+        sums = [psum.tile([P, 2, hi - lo], F32, name="sums%d" % j, tag="bank%d" % j) for j, (lo, hi) in enumerate(CHUNKS[:2])]
         acc2 = [psum.tile([P, P], F32, name="acc2%d" % m) for m in range(2)]
         u_words = u[:].rearrange("p n t -> p (n t)").bitcast(F32)
         pair_words = pairs[:].rearrange("p h n e -> p h (n e)").bitcast(F32)
-        back = [psum.tile([P, 2, hi - lo], F32, name="back%d" % lo) for lo, hi in CHUNKS[:2]]
+        back = psum.tile([P, EARLY], F32, name="back")
+        turned_words = turned[:].rearrange("s n e -> s (n e)").bitcast(F32)
         out_v = out[0].rearrange("(m p) n -> p m n", p=P)
 
         def cos_product(t, lo, hi):
@@ -83,22 +83,24 @@ def tile_attend_pre_rope_f_topk_kernel(tc, qT, kT, cT, wT, offs, offs2, out):
             w = wneg[t // 2] if t % 2 else wg[t // 2]
             nc.vector.tensor_tensor(kw[:, t ^ 1, lo:hi], kp[t][:].indirect(tok[:, lo // 16 : hi // 16]), w[:, lo:hi], MULT)
 
-        def early_sum(t):
-            for b in range(EARLY // P):
-                cols = slice(b * P, (b + 1) * P)
-                nc.tensor.matmul(sums[t][:, cols], kc[:, t, cols], ident[:], start=True, stop=False, is_transpose=True)
-                nc.tensor.matmul(sums[t][:, cols], kw[:, t, cols], ident[:], start=False, stop=True, is_transpose=True)
-            nc.scalar.copy(turned[:, t, :], sums[t][:])
-
-        def early_back(j):
+        def early_sum(t, j):
             lo, hi = CHUNKS[j]
-            for t in (1, 0):
-                for c in range(lo, hi, P):
-                    nc.tensor.transpose(back[j][:, t, c - lo : c - lo + P], turned[:, t, c : c + P], ident[:])
+            for c in range(lo, hi, P):
+                dst = sums[j][:, t, c - lo : c - lo + P]
+                nc.tensor.matmul(dst, kc[:, t, c : c + P], ident[:], start=True, stop=False, is_transpose=True)
+                nc.tensor.matmul(dst, kw[:, t, c : c + P], ident[:], start=False, stop=True, is_transpose=True)
+
+        def early_round(j):
+            lo, hi = CHUNKS[j]
             nc.scalar.copy(
-                pairs[:, 0, lo:hi, :].rearrange("p (c i) e -> p c e i", i=4),
-                back[j][:].rearrange("p e (c i) -> p c e i", i=4),
+                turned[:, lo:hi, :].rearrange("s (c i) e -> s c e i", i=4),
+                sums[j][:].rearrange("s e (c i) -> s c e i", i=4),
             )
+
+        def early_back():
+            for c in range(0, EARLY, P):
+                nc.tensor.transpose(back[:, c : c + P], turned_words[:, c : c + P], ident[:])
+            nc.scalar.copy(pair_words[:, 0, :], back[:])
 
         def add_late_pair(j):
             cols = slice(*CHUNKS[j])
@@ -151,12 +153,14 @@ def tile_attend_pre_rope_f_topk_kernel(tc, qT, kT, cT, wT, offs, offs2, out):
         for t in range(PACK - 1):
             cos_product(t, 0, N)
             if t == 1:
-                early_sum(1)
+                early_sum(1, 0)
+                early_sum(1, 1)
             sin_product(t, 0, N)
             if t == 1:
-                early_sum(0)
-                early_back(0)
-                early_back(1)
+                for j in range(2):
+                    early_sum(0, j)
+                    early_round(j)
+                early_back()
 
         nc.scalar.copy(
             qb[:].rearrange("p (c i) t -> p c t i", i=2),
@@ -170,12 +174,14 @@ def tile_attend_pre_rope_f_topk_kernel(tc, qT, kT, cT, wT, offs, offs2, out):
         add_late_pair(0)
         sin_product(last, 256, N)
         nc.vector.quantize_mx(out=q_codes[:].bitcast(FP8X4), scales=q_scales[:], in_=qb[:].rearrange("p n t -> p (n t)"))
-        quantize(0)
         add_late_pair(1)
-        scores(0, [acc0[:, 0, :], acc0[:, 1, :]])
+        quantize(0)
+        acc0 = [psum.tile([P, 256], F32, name="acc0%d" % m) for m in range(2)]
+        scores(0, [acc0[0][:], acc0[1][:]])
         add(2)
-        nc.scalar.copy(res0[:], acc0[:])
-        nc.sync.dma_start(out=out_v[:, :, 0:256], in_=res0[:])
+        for m in range(2):
+            nc.scalar.copy(res0[:, m, :], acc0[m][:])
+            nc.sync.dma_start(out=out_v[:, m, 0:256], in_=res0[:, m, :])
         quantize(1)
         quantize(2)
         acc1 = [psum.tile([P, P], F32, name="acc1%d" % m, tag="bank%d" % m) for m in range(2)]

@@ -19,8 +19,8 @@ COPY = mybir.ActivationFunctionType.Copy
 
 P = 128
 PACK = 4
-CHUNKS = ((0, 256), (256, 384), (384, 512))
-EARLY = 384
+CHUNKS = N // P
+TURNED = 2
 
 
 def tile_attend_pre_rope_f_topk_kernel(tc, qT, kT, cT, wT, offs, offs2, out):
@@ -34,7 +34,7 @@ def tile_attend_pre_rope_f_topk_kernel(tc, qT, kT, cT, wT, offs, offs2, out):
         kp = [pool.tile([P, T], F32, name="kp%d" % t) for t in range(PACK)]
         cp = [pool.tile([P, POS], F32, name="cp%d" % h) for h in range(2)]
         wp = [pool.tile([P, POS], F32, name="wp%d" % h) for h in range(2)]
-        q_raw = pool.tile([P, PACK, NQ], F32, name="q_raw")
+        q_raw = pool.tile([P, PACK, NQ], F32, name="q_raw", tag="q_raw")
         kv = kT.rearrange("(p t) n -> p t n", t=PACK)
         cv = cT.rearrange("(p t) n -> p t n", t=PACK)
         wv = wT.rearrange("(p t) n -> p t n", t=PACK)
@@ -45,9 +45,10 @@ def tile_attend_pre_rope_f_topk_kernel(tc, qT, kT, cT, wT, offs, offs2, out):
         nc.sync.dma_start(out=wp[1][:], in_=wv[:, 2, :])
         nc.sync.dma_start(out=cp[1][:], in_=cv[:, 2, :])
         nc.sync.dma_start(tok[:], offs)
-        for t in range(PACK):
+        for t in range(PACK - 1):
             nc.sync.dma_start(out=kp[t][:], in_=kv[:, t, :])
         nc.sync.dma_start(out=q_raw[:], in_=qT[0].rearrange("(p t) n -> p t n", t=PACK))
+        nc.sync.dma_start(out=kp[PACK - 1][:], in_=kv[:, PACK - 1, :])
 
         ident = pool.tile([P, P], F32, name="ident")
         make_identity(nc, ident[:])
@@ -57,23 +58,15 @@ def tile_attend_pre_rope_f_topk_kernel(tc, qT, kT, cT, wT, offs, offs2, out):
         wneg = [pool.tile([P, N], F32, name="wneg%d" % h) for h in range(2)]
         kc = pool.tile([P, PACK, N], F32, name="kc")
         kw = pool.tile([P, PACK, N], F32, name="kw")
-        turned = pool.tile([P, EARLY, 2], BF16, name="turned", align_bytes=64)
-        pairs = pool.tile([P, 2, EARLY, 2], BF16, name="pairs", align_bytes=64)
-        u = pool.tile([P, N, PACK], BF16, name="u", align_bytes=64)
-        u_codes = pool.tile([P, N], U32, name="u_codes", align_bytes=64)
-        u_scales = pool.tile([P, N], U8, name="u_scales", align_bytes=64)
-        qb = pool.tile([P, NQ, PACK], BF16, name="qb", align_bytes=64)
+        u = [pool.tile([P, P, PACK], BF16, name="u%d" % j, tag="u%d" % j, align_bytes=64) for j in range(CHUNKS)]
+        u_words = [u[j][:].rearrange("p n t -> p (n t)").bitcast(F32).rearrange("p (n h) -> p n h", h=2) for j in range(CHUNKS)]
+        qb = pool.tile([P, NQ, PACK], BF16, name="qb", tag="qb", align_bytes=64)
         q_codes = pool.tile([P, NQ], U32, name="q_codes", align_bytes=64)
         q_scales = pool.tile([P, NQ], U8, name="q_scales", align_bytes=64)
-        res0 = pool.tile([P, 2, 256], F32, name="res0")
-        res1 = pool.tile([P, 2, P], F32, name="res1")
-        res2 = pool.tile([P, 2, P], F32, name="res2")
-        sums = [psum.tile([P, 2, hi - lo], F32, name="sums%d" % j, tag="bank%d" % j) for j, (lo, hi) in enumerate(CHUNKS[:2])]
-        acc2 = [psum.tile([P, P], F32, name="acc2%d" % m) for m in range(2)]
-        u_words = u[:].rearrange("p n t -> p (n t)").bitcast(F32)
-        pair_words = pairs[:].rearrange("p h n e -> p h (n e)").bitcast(F32)
-        back = psum.tile([P, EARLY], F32, name="back")
-        turned_words = turned[:].rearrange("s n e -> s (n e)").bitcast(F32)
+        res = {}
+        sums0 = [psum.tile([P, 2, 2 * P], F32, name="sums0%d" % g, tag="bank%d" % g) for g in range(2)]
+        back = [psum.tile([P, 2, P], F32, name="back%d" % j) for j in range(TURNED)]
+        back_rest = psum.tile([P, CHUNKS - TURNED, P], F32, name="back_rest", tag="bank4")
         out_v = out[0].rearrange("(m p) n -> p m n", p=P)
 
         def cos_product(t, lo, hi):
@@ -83,113 +76,153 @@ def tile_attend_pre_rope_f_topk_kernel(tc, qT, kT, cT, wT, offs, offs2, out):
             w = wneg[t // 2] if t % 2 else wg[t // 2]
             nc.vector.tensor_tensor(kw[:, t ^ 1, lo:hi], kp[t][:].indirect(tok[:, lo // 16 : hi // 16]), w[:, lo:hi], MULT)
 
-        def early_sum(t, j):
-            lo, hi = CHUNKS[j]
-            for c in range(lo, hi, P):
-                dst = sums[j][:, t, c - lo : c - lo + P]
-                nc.tensor.matmul(dst, kc[:, t, c : c + P], ident[:], start=True, stop=False, is_transpose=True)
-                nc.tensor.matmul(dst, kw[:, t, c : c + P], ident[:], start=False, stop=True, is_transpose=True)
+        def turn(dst, src, start, stop):
+            nc.tensor.matmul(dst, src, ident[:], start=start, stop=stop, is_transpose=True)
 
-        def early_round(j):
-            lo, hi = CHUNKS[j]
+        def early_sum(t, g):
+            for c in range(2):
+                cols = slice((2 * g + c) * P, (2 * g + c + 1) * P)
+                dst = sums0[g][:, t, c * P : (c + 1) * P]
+                turn(dst, kc[:, t, cols], True, False)
+                turn(dst, kw[:, t, cols], False, True)
+
+        def round_turned(dst, src):
             nc.scalar.copy(
-                turned[:, lo:hi, :].rearrange("s (c i) e -> s c e i", i=4),
-                sums[j][:].rearrange("s e (c i) -> s c e i", i=4),
+                dst.rearrange("s (c i) e -> s c e i", i=4),
+                src.rearrange("s e (c i) -> s c e i", i=4),
             )
 
-        def early_back():
-            for c in range(0, EARLY, P):
-                nc.tensor.transpose(back[:, c : c + P], turned_words[:, c : c + P], ident[:])
-            nc.scalar.copy(pair_words[:, 0, :], back[:])
+        def early_back(j):
+            dst = back[j][:, 0, :] if j < TURNED else back_rest[:, j - TURNED, :]
+            nc.tensor.transpose(dst, turned0_words[:, j * P : (j + 1) * P], ident[:])
 
         def add_late_pair(j):
-            cols = slice(*CHUNKS[j])
+            cols = slice(j * P, (j + 1) * P)
             nc.vector.tensor_tensor(
-                pairs[:, 1, cols, :].rearrange("p (c i) e -> p c e i", i=4),
-                kc[:, 2:4, cols].rearrange("p e (c i) -> p c e i", i=4),
-                kw[:, 2:4, cols].rearrange("p e (c i) -> p c e i", i=4),
-                ADD,
-            )
-            nc.scalar.copy(
-                u_words[:, 2 * cols.start : 2 * cols.stop].rearrange("p (n h) -> p n h", h=2),
-                pair_words[:, :, cols].rearrange("p h n -> p n h"),
-            )
-
-        def add(j):
-            cols = slice(*CHUNKS[j])
-            nc.vector.tensor_tensor(
-                u[:, cols, :].rearrange("p (c i) t -> p c t i", i=2),
-                kc[:, :, cols].rearrange("p t (c i) -> p c t i", i=2),
-                kw[:, :, cols].rearrange("p t (c i) -> p c t i", i=2),
+                u[j][:, :, 2:4].rearrange("p (c i) e -> p c e i", i=2),
+                kc[:, 2:4, cols].rearrange("p e (c i) -> p c e i", i=2),
+                kw[:, 2:4, cols].rearrange("p e (c i) -> p c e i", i=2),
                 ADD,
             )
 
-        def quantize(j):
-            cols = slice(*CHUNKS[j])
+        u_codes = {}
+        u_scales = {}
+
+        def quantize(j, tag=None):
+            u_codes[j] = pool.tile([P, P], U32, name="u_codes%d" % j, tag=tag or "u_codes%d" % j, align_bytes=64)
+            u_scales[j] = pool.tile([P, P], U8, name="u_scales%d" % j, align_bytes=64)
             nc.vector.quantize_mx(
-                out=u_codes[:, cols].bitcast(FP8X4),
-                scales=u_scales[:, cols],
-                in_=u[:, cols, :].rearrange("p n t -> p (n t)"),
+                out=u_codes[j][:].bitcast(FP8X4),
+                scales=u_scales[j][:],
+                in_=u[j][:].rearrange("p n t -> p (n t)"),
             )
 
         def scores(j, accs):
-            cols = slice(*CHUNKS[j])
             for m in range(2):
                 rows = slice(m * P, (m + 1) * P)
                 nc.tensor.matmul_mx(
                     out=accs[m],
                     lhsT=q_codes[:, rows].bitcast(FP8X4),
                     lhsT_scale=q_scales[:, rows],
-                    rhs=u_codes[:, cols].bitcast(FP8X4),
-                    rhs_scale=u_scales[:, cols],
+                    rhs=u_codes[j][:].bitcast(FP8X4),
+                    rhs_scale=u_scales[j][:],
                     start=True,
                     stop=True,
                 )
+
+        def finish(j, bank, engine_copy, tag):
+            res[j] = pool.tile([P, 2, P], F32, name="res%d" % j, tag=tag, align_bytes=64)
+            acc = psum.tile([P, 2, P], F32, name="acc%d" % j, tag="bank%d" % bank)
+            scores(j, [acc[:, 0, :], acc[:, 1, :]])
+            engine_copy(res[j][:], acc[:])
+            nc.sync.dma_start(out=out_v[:, :, j * P : (j + 1) * P], in_=res[j][:])
+
+        def finish_split(j, banks):
+            res[j] = pool.tile([P, 2, P], F32, name="res%d" % j)
+            accs = [psum.tile([P, P], F32, name="acc%d%d" % (j, m), tag="bank%d" % banks[m]) for m in range(2)]
+            scores(j, [accs[0][:], accs[1][:]])
+            nc.scalar.copy(res[j][:, 0, :], accs[0][:])
+            nc.vector.tensor_copy(res[j][:, 1, :], accs[1][:])
+            nc.sync.dma_start(out=out_v[:, :, j * P : (j + 1) * P], in_=res[j][:])
 
         for h in range(2):
             nc.vector.tensor_copy(wg[h][:], wp[h][:].indirect(pos[:]))
             nc.scalar.activation(wneg[h][:], wg[h][:], COPY, scale=-1.0)
             nc.vector.tensor_copy(cg[h][:], cp[h][:].indirect(pos[:]))
-        for t in range(PACK - 1):
-            cos_product(t, 0, N)
-            if t == 1:
-                early_sum(1, 0)
-                early_sum(1, 1)
-            sin_product(t, 0, N)
-            if t == 1:
-                for j in range(2):
-                    early_sum(0, j)
-                    early_round(j)
-                early_back()
-
+        cos_product(0, 0, N)
+        sin_product(0, 0, N)
+        cos_product(1, 0, N)
+        early_sum(1, 1)
+        early_sum(1, 0)
+        sin_product(1, 0, N)
         nc.scalar.copy(
             qb[:].rearrange("p (c i) t -> p c t i", i=2),
             q_raw[:].rearrange("p t (c i) -> p c t i", i=2),
         )
+        turned0 = pool.tile([P, N, 2], BF16, name="turned0", tag="q_raw")
+        turned0_words = turned0[:].rearrange("s n e -> s (n e)").bitcast(F32)
+        for g in (1, 0):
+            early_sum(0, g)
+            round_turned(turned0[:, 2 * g * P : 2 * (g + 1) * P, :], sums0[g][:])
+        for j in range(TURNED, CHUNKS):
+            early_back(j)
+        for j in range(TURNED, CHUNKS):
+            nc.scalar.copy(u_words[j][:, :, 0], back_rest[:, j - TURNED, :])
+        for j in range(TURNED):
+            early_back(j)
+        sums1 = {}
+
+        def open_late_sum(j):
+            cols = slice(j * P, (j + 1) * P)
+            sums1[j] = psum.tile([P, 2, P], F32, name="sums1%d" % j, tag="bank%d" % (2 + j % 2))
+            turn(sums1[j][:, 0, :], kc[:, 2, cols], True, False)
+            turn(sums1[j][:, 1, :], kw[:, 3, cols], False, False)
+
+        cos_product(2, 0, N)
+        sin_product(2, 0, N)
+        for j in range(2):
+            open_late_sum(j)
+
+
+        nc.vector.quantize_mx(out=q_codes[:].bitcast(FP8X4), scales=q_scales[:], in_=qb[:].rearrange("p n t -> p (n t)"))
 
         last = PACK - 1
-        cos_product(last, 0, 256)
-        sin_product(last, 0, 256)
-        cos_product(last, 256, N)
-        add_late_pair(0)
-        sin_product(last, 256, N)
-        nc.vector.quantize_mx(out=q_codes[:].bitcast(FP8X4), scales=q_scales[:], in_=qb[:].rearrange("p n t -> p (n t)"))
-        add_late_pair(1)
-        quantize(0)
-        acc0 = [psum.tile([P, 256], F32, name="acc0%d" % m) for m in range(2)]
-        scores(0, [acc0[0][:], acc0[1][:]])
-        add(2)
-        for m in range(2):
-            nc.scalar.copy(res0[:, m, :], acc0[m][:])
-            nc.sync.dma_start(out=out_v[:, m, 0:256], in_=res0[:, m, :])
-        quantize(1)
+        turned1 = {}
+
+        def late_products(j):
+            cos_product(last, j * P, (j + 1) * P)
+            sin_product(last, j * P, (j + 1) * P)
+
+        def late_sum(j):
+            cols = slice(j * P, (j + 1) * P)
+            turn(sums1[j][:, 1, :], kc[:, 3, cols], False, False)
+            turn(sums1[j][:, 0, :], kw[:, 2, cols], False, True)
+
+        def late_round(j):
+            turned1[j] = pool.tile([P, P, 2], BF16, name="turned1%d" % j, tag="turned1%d" % j, align_bytes=64)
+            round_turned(turned1[j][:], sums1[j][:])
+
+        def late_back(j):
+            nc.tensor.transpose(back[j][:, 1, :], turned1[j][:].rearrange("s n e -> s (n e)").bitcast(F32), ident[:])
+            nc.scalar.copy(u_words[j], back[j][:].rearrange("p h n -> p n h"))
+
+        late_products(0)
+        late_products(1)
+        late_sum(0)
+        late_sum(1)
+        late_round(0)
+        late_round(1)
+        late_back(0)
+        late_back(1)
+        late_products(2)
+        add_late_pair(2)
+        late_products(3)
         quantize(2)
-        acc1 = [psum.tile([P, P], F32, name="acc1%d" % m, tag="bank%d" % m) for m in range(2)]
-        scores(1, [acc1[0][:], acc1[1][:]])
-        scores(2, [acc2[0][:], acc2[1][:]])
-        nc.scalar.copy(res1[:, 0, :], acc1[0][:])
-        nc.vector.tensor_copy(res1[:, 1, :], acc1[1][:])
-        nc.sync.dma_start(out=out_v[:, :, 256:384], in_=res1[:])
-        nc.scalar.copy(res2[:, 0, :], acc2[0][:])
-        nc.vector.tensor_copy(res2[:, 1, :], acc2[1][:])
-        nc.sync.dma_start(out=out_v[:, :, 384:N], in_=res2[:])
+        finish(2, 0, nc.scalar.copy, "turned11")
+        add_late_pair(3)
+        quantize(0)
+        finish(0, 1, nc.scalar.copy, "res0")
+        quantize(3, "u0")
+        quantize(1)
+        finish(3, 4, nc.vector.tensor_copy, "u1")
+        finish_split(1, (2, 5))

@@ -34,7 +34,7 @@ def tile_attend_pre_rope_f_topk_kernel(tc, qT, kT, cT, wT, offs, offs2, out):
         kp = [pool.tile([P, T], F32, name="kp%d" % t) for t in range(PACK)]
         cp = [pool.tile([P, POS], F32, name="cp%d" % h) for h in range(2)]
         wp = [pool.tile([P, POS], F32, name="wp%d" % h) for h in range(2)]
-        q_raw = pool.tile([P, PACK, NQ], F32, name="q_raw", tag="q_raw")
+        q_raw = pool.tile([P, PACK, NQ], F32, name="q_raw", tag="q_raw", align_bytes=64)
         kv = kT.rearrange("(p t) n -> p t n", t=PACK)
         cv = cT.rearrange("(p t) n -> p t n", t=PACK)
         wv = wT.rearrange("(p t) n -> p t n", t=PACK)
@@ -42,13 +42,14 @@ def tile_attend_pre_rope_f_topk_kernel(tc, qT, kT, cT, wT, offs, offs2, out):
         nc.sync.dma_start(out=wp[0][:], in_=wv[:, 0, :])
         nc.sync.dma_start(pos[:], offs2)
         nc.sync.dma_start(out=cp[0][:], in_=cv[:, 0, :])
+        nc.sync.dma_start(tok[:], offs)
+        nc.sync.dma_start(out=kp[0][:], in_=kv[:, 0, :])
+        nc.sync.dma_start(out=kp[1][:], in_=kv[:, 1, :])
         nc.sync.dma_start(out=wp[1][:], in_=wv[:, 2, :])
         nc.sync.dma_start(out=cp[1][:], in_=cv[:, 2, :])
-        nc.sync.dma_start(tok[:], offs)
-        for t in range(PACK - 1):
-            nc.sync.dma_start(out=kp[t][:], in_=kv[:, t, :])
+        nc.sync.dma_start(out=kp[2][:], in_=kv[:, 2, :])
+        nc.sync.dma_start(out=kp[3][:], in_=kv[:, 3, :])
         nc.sync.dma_start(out=q_raw[:], in_=qT[0].rearrange("(p t) n -> p t n", t=PACK))
-        nc.sync.dma_start(out=kp[PACK - 1][:], in_=kv[:, PACK - 1, :])
 
         ident = pool.tile([P, P], F32, name="ident")
         make_identity(nc, ident[:])
@@ -56,35 +57,47 @@ def tile_attend_pre_rope_f_topk_kernel(tc, qT, kT, cT, wT, offs, offs2, out):
         cg = [pool.tile([P, N], F32, name="cg%d" % h) for h in range(2)]
         wg = [pool.tile([P, N], F32, name="wg%d" % h) for h in range(2)]
         wneg = [pool.tile([P, N], F32, name="wneg%d" % h) for h in range(2)]
-        kc = pool.tile([P, PACK, N], F32, name="kc")
-        kw = pool.tile([P, PACK, N], F32, name="kw")
+        kg = [pool.tile([P, N], F32, name="kg%d" % h) for h in range(2)]
+        kc = pool.tile([P, 2, N], F32, name="kc")
+        kw = pool.tile([P, 2, N], F32, name="kw")
+        first = pool.tile([P, 2, N], F32, name="first")
+        turned0 = pool.tile([P, N, 2], BF16, name="turned0")
+        turned0_words = turned0[:].rearrange("s n e -> s (n e)").bitcast(F32)
+        shared = pool.tile([P, 5 * P], F32, name="shared", align_bytes=64)
+        qb = shared[:, 0 : 4 * P].bitcast(BF16)
+        late_tiles = [pool.tile([P, 2, P], F32, name="late%d" % j) for j in range(3)]
+        late = [late_tiles[j][:] for j in range(3)] + [shared[:].rearrange("p (a b) -> p a b", b=P)[:, 0:5:4, :]]
         u = [pool.tile([P, P, PACK], BF16, name="u%d" % j, tag="u%d" % j, align_bytes=64) for j in range(CHUNKS)]
         u_words = [u[j][:].rearrange("p n t -> p (n t)").bitcast(F32).rearrange("p (n h) -> p n h", h=2) for j in range(CHUNKS)]
-        qb = pool.tile([P, NQ, PACK], BF16, name="qb", tag="qb", align_bytes=64)
         q_codes = pool.tile([P, NQ], U32, name="q_codes", align_bytes=64)
         q_scales = pool.tile([P, NQ], U8, name="q_scales", align_bytes=64)
         res = {}
         sums0 = [psum.tile([P, 2, 2 * P], F32, name="sums0%d" % g, tag="bank%d" % g) for g in range(2)]
-        back = [psum.tile([P, 2, P], F32, name="back%d" % j) for j in range(TURNED)]
+        back = [psum.tile([P, 2, P], F32, name="back%d" % j, tag="bank%d" % (5 + j)) for j in range(TURNED)]
         back_rest = psum.tile([P, CHUNKS - TURNED, P], F32, name="back_rest", tag="bank4")
         out_v = out[0].rearrange("(m p) n -> p m n", p=P)
 
-        def cos_product(t, lo, hi):
-            nc.vector.tensor_tensor(kc[:, t, lo:hi], kp[t][:].indirect(tok[:, lo // 16 : hi // 16]), cg[t // 2][:, lo:hi], MULT)
+        def gather_table(dst, table):
+            nc.vector.tensor_copy(dst[:], table[:].indirect(pos[:]))
 
-        def sin_product(t, lo, hi):
+        def negate(h):
+            nc.scalar.activation(wneg[h][:], wg[h][:], COPY, scale=-1.0)
+
+        def cos_product(t, lo, hi, dst):
+            nc.vector.tensor_tensor(dst, kp[t][:].indirect(tok[:, lo // 16 : hi // 16]), cg[t // 2][:, lo:hi], MULT)
+
+        def sin_product(t, lo, hi, dst):
             w = wneg[t // 2] if t % 2 else wg[t // 2]
-            nc.vector.tensor_tensor(kw[:, t ^ 1, lo:hi], kp[t][:].indirect(tok[:, lo // 16 : hi // 16]), w[:, lo:hi], MULT)
+            nc.vector.tensor_tensor(dst, kp[t][:].indirect(tok[:, lo // 16 : hi // 16]), w[:, lo:hi], MULT)
 
         def turn(dst, src, start, stop):
             nc.tensor.matmul(dst, src, ident[:], start=start, stop=stop, is_transpose=True)
 
-        def early_sum(t, g):
-            for c in range(2):
-                cols = slice((2 * g + c) * P, (2 * g + c + 1) * P)
-                dst = sums0[g][:, t, c * P : (c + 1) * P]
-                turn(dst, kc[:, t, cols], True, False)
-                turn(dst, kw[:, t, cols], False, True)
+        def early_sum(src, t, start, stop):
+            for g in (1, 0):
+                for c in range(2):
+                    cols = slice((2 * g + c) * P, (2 * g + c + 1) * P)
+                    turn(sums0[g][:, t, c * P : (c + 1) * P], src[:, t, cols], start and c == 0, stop and c == 1)
 
         def round_turned(dst, src):
             nc.scalar.copy(
@@ -100,21 +113,37 @@ def tile_attend_pre_rope_f_topk_kernel(tc, qT, kT, cT, wT, offs, offs2, out):
             cols = slice(j * P, (j + 1) * P)
             nc.vector.tensor_tensor(
                 u[j][:, :, 2:4].rearrange("p (c i) e -> p c e i", i=2),
-                kc[:, 2:4, cols].rearrange("p e (c i) -> p c e i", i=2),
-                kw[:, 2:4, cols].rearrange("p e (c i) -> p c e i", i=2),
+                first[:, :, cols].rearrange("p e (c i) -> p c e i", i=2),
+                late[j].rearrange("p e (c i) -> p c e i", i=2),
                 ADD,
             )
 
         u_codes = {}
         u_scales = {}
 
-        def quantize(j, tag=None):
-            u_codes[j] = pool.tile([P, P], U32, name="u_codes%d" % j, tag=tag or "u_codes%d" % j, align_bytes=64)
-            u_scales[j] = pool.tile([P, P], U8, name="u_scales%d" % j, align_bytes=64)
+        def quantize(j, tag=None, scales=None):
+            codes = pool.tile([P, P], U32, name="u_codes%d" % j, tag=tag or "u_codes%d" % j, align_bytes=64)
+            u_codes[j] = codes[:]
+            if scales is None:
+                own = pool.tile([P, P], U8, name="u_scales%d" % j, align_bytes=64)
+                scales = own[:]
+            u_scales[j] = scales
             nc.vector.quantize_mx(
-                out=u_codes[j][:].bitcast(FP8X4),
-                scales=u_scales[j][:],
+                out=u_codes[j].bitcast(FP8X4),
+                scales=u_scales[j],
                 in_=u[j][:].rearrange("p n t -> p (n t)"),
+            )
+
+        def quantize_queries(m):
+            rows = slice(m * P, (m + 1) * P)
+            nc.vector.quantize_mx(
+                out=q_codes[:, rows].bitcast(FP8X4), scales=q_scales[:, rows], in_=qb[:, m * PACK * P : (m + 1) * PACK * P]
+            )
+
+        def cast_queries():
+            nc.scalar.copy(
+                qb.rearrange("p (c i t) -> p c t i", i=2, t=PACK),
+                q_raw[:].rearrange("p t (c i) -> p c t i", i=2),
             )
 
         def scores(j, accs):
@@ -124,8 +153,8 @@ def tile_attend_pre_rope_f_topk_kernel(tc, qT, kT, cT, wT, offs, offs2, out):
                     out=accs[m],
                     lhsT=q_codes[:, rows].bitcast(FP8X4),
                     lhsT_scale=q_scales[:, rows],
-                    rhs=u_codes[j][:].bitcast(FP8X4),
-                    rhs_scale=u_scales[j][:],
+                    rhs=u_codes[j].bitcast(FP8X4),
+                    rhs_scale=u_scales[j],
                     start=True,
                     stop=True,
                 )
@@ -145,84 +174,83 @@ def tile_attend_pre_rope_f_topk_kernel(tc, qT, kT, cT, wT, offs, offs2, out):
             nc.vector.tensor_copy(res[j][:, 1, :], accs[1][:])
             nc.sync.dma_start(out=out_v[:, :, j * P : (j + 1) * P], in_=res[j][:])
 
-        for h in range(2):
-            nc.vector.tensor_copy(wg[h][:], wp[h][:].indirect(pos[:]))
-            nc.scalar.activation(wneg[h][:], wg[h][:], COPY, scale=-1.0)
-            nc.vector.tensor_copy(cg[h][:], cp[h][:].indirect(pos[:]))
-        cos_product(0, 0, N)
-        sin_product(0, 0, N)
-        cos_product(1, 0, N)
-        early_sum(1, 1)
-        early_sum(1, 0)
-        sin_product(1, 0, N)
-        nc.scalar.copy(
-            qb[:].rearrange("p (c i) t -> p c t i", i=2),
-            q_raw[:].rearrange("p t (c i) -> p c t i", i=2),
-        )
-        turned0 = pool.tile([P, N, 2], BF16, name="turned0", tag="q_raw")
-        turned0_words = turned0[:].rearrange("s n e -> s (n e)").bitcast(F32)
-        for g in (1, 0):
-            early_sum(0, g)
-            round_turned(turned0[:, 2 * g * P : 2 * (g + 1) * P, :], sums0[g][:])
-        for j in range(TURNED, CHUNKS):
-            early_back(j)
-        for j in range(TURNED, CHUNKS):
-            nc.scalar.copy(u_words[j][:, :, 0], back_rest[:, j - TURNED, :])
-        for j in range(TURNED):
-            early_back(j)
-        sums1 = {}
-
-        def open_late_sum(j):
-            cols = slice(j * P, (j + 1) * P)
-            sums1[j] = psum.tile([P, 2, P], F32, name="sums1%d" % j, tag="bank%d" % (2 + j % 2))
-            turn(sums1[j][:, 0, :], kc[:, 2, cols], True, False)
-            turn(sums1[j][:, 1, :], kw[:, 3, cols], False, False)
-
-        cos_product(2, 0, N)
-        sin_product(2, 0, N)
-        for j in range(2):
-            open_late_sum(j)
-
-
-        nc.vector.quantize_mx(out=q_codes[:].bitcast(FP8X4), scales=q_scales[:], in_=qb[:].rearrange("p n t -> p (n t)"))
+        def first_pair_sums():
+            for g in (1, 0):
+                round_turned(turned0[:, 2 * g * P : 2 * (g + 1) * P, :], sums0[g][:])
+            for j in range(TURNED, CHUNKS):
+                early_back(j)
+            for j in range(TURNED, CHUNKS):
+                nc.scalar.copy(u_words[j][:, :, 0], back_rest[:, j - TURNED, :])
+            for j in range(TURNED):
+                early_back(j)
 
         last = PACK - 1
-        turned1 = {}
 
-        def late_products(j):
-            cos_product(last, j * P, (j + 1) * P)
-            sin_product(last, j * P, (j + 1) * P)
+        def late_cos(j):
+            cos_product(last, j * P, (j + 1) * P, late[j][:, 1, :])
+
+        def late_sin(j):
+            sin_product(last, j * P, (j + 1) * P, late[j][:, 0, :])
 
         def late_sum(j):
-            cols = slice(j * P, (j + 1) * P)
-            turn(sums1[j][:, 1, :], kc[:, 3, cols], False, False)
-            turn(sums1[j][:, 0, :], kw[:, 2, cols], False, True)
+            turn(sums1[j][:, 1, :], late[j][:, 1, :], False, False)
+            turn(sums1[j][:, 0, :], late[j][:, 0, :], False, True)
 
         def late_round(j):
-            turned1[j] = pool.tile([P, P, 2], BF16, name="turned1%d" % j, tag="turned1%d" % j, align_bytes=64)
-            round_turned(turned1[j][:], sums1[j][:])
+            round_turned(turned1[:, 2 * j * P : 2 * (j + 1) * P].rearrange("s (n e) -> s n e", e=2), sums1[j][:])
 
         def late_back(j):
-            nc.tensor.transpose(back[j][:, 1, :], turned1[j][:].rearrange("s n e -> s (n e)").bitcast(F32), ident[:])
+            nc.tensor.transpose(back[j][:, 1, :], turned1[:, 2 * j * P : 2 * (j + 1) * P].bitcast(F32), ident[:])
             nc.scalar.copy(u_words[j], back[j][:].rearrange("p h n -> p n h"))
 
-        late_products(0)
-        late_products(1)
+        gather_table(wg[0], wp[0])
+        negate(0)
+        gather_table(cg[0], cp[0])
+        nc.vector.tensor_copy(kg[0][:], kp[0][:].indirect(tok[:]))
+        nc.vector.tensor_tensor(kw[:, 1, :], kg[0][:], wg[0][:], MULT)
+        early_sum(kw, 1, True, False)
+        nc.gpsimd.tensor_tensor(kc[:, 0, :], kg[0][:], cg[0][:], MULT)
+        early_sum(kc, 0, False, False)
+        nc.vector.tensor_copy(kg[1][:], kp[1][:].indirect(tok[:]))
+        nc.gpsimd.tensor_tensor(kc[:, 1, :], kg[1][:], cg[0][:], MULT)
+        early_sum(kc, 1, False, False)
+        nc.gpsimd.tensor_tensor(kw[:, 0, :], kg[1][:], wneg[0][:], MULT)
+        early_sum(kw, 0, False, True)
+        first_pair_sums()
+        gather_table(wg[1], wp[1])
+        negate(1)
+        gather_table(cg[1], cp[1])
+        sums1 = [psum.tile([P, 2, P], F32, name="sums1%d" % j, tag=("bank4", "bank0")[j]) for j in range(TURNED)]
+        cos_product(2, 0, N, first[:, 0, :])
+        sin_product(2, 0, N, first[:, 1, :])
+        for j in range(TURNED):
+            cols = slice(j * P, (j + 1) * P)
+            turn(sums1[j][:, 0, :], first[:, 0, cols], True, False)
+            turn(sums1[j][:, 1, :], first[:, 1, cols], False, False)
+        cast_queries()
+        turned1 = pool.tile([P, 2 * TURNED * P], BF16, name="turned1", tag="q_raw", align_bytes=64)
+        for j in range(TURNED):
+            late_cos(j)
+            late_sin(j)
         late_sum(0)
         late_sum(1)
         late_round(0)
         late_round(1)
         late_back(0)
         late_back(1)
-        late_products(2)
+        late_cos(2)
+        late_sin(2)
+        late_cos(3)
         add_late_pair(2)
-        late_products(3)
-        quantize(2)
-        finish(2, 0, nc.scalar.copy, "turned11")
+        quantize_queries(0)
+        quantize_queries(1)
+        late_sin(3)
+        quantize(2, scales=q_scales[4:P, 0:P])
+        finish(2, 0, nc.scalar.copy, "res2")
         add_late_pair(3)
         quantize(0)
         finish(0, 1, nc.scalar.copy, "res0")
-        quantize(3, "u0")
+        quantize(3, "q_raw")
         quantize(1)
-        finish(3, 4, nc.vector.tensor_copy, "u1")
-        finish_split(1, (2, 5))
+        finish(3, 2, nc.vector.tensor_copy, "u1")
+        finish_split(1, (3, 7))

@@ -20,13 +20,16 @@ COPY = mybir.ActivationFunctionType.Copy
 P = 128
 PACK = 4
 CHUNKS = N // P
-TURNED = 2
+HALF = N // 2
+TURNED = (0, 1)
+ADDED = (2, 3)
 
 
 def tile_attend_pre_rope_f_topk_kernel(tc, qT, kT, cT, wT, offs, offs2, out):
     nc = tc.nc
     with ExitStack() as ctx:
         pool = ctx.enter_context(tc.tile_pool(name="held", bufs=1))
+        reused = ctx.enter_context(tc.tile_pool(name="reused", bufs=1))
         psum = ctx.enter_context(tc.psum_pool(name="psum", bufs=1))
 
         tok = pool.tile([P, N // 16], U16, name="tok")
@@ -34,7 +37,7 @@ def tile_attend_pre_rope_f_topk_kernel(tc, qT, kT, cT, wT, offs, offs2, out):
         kp = [pool.tile([P, T], F32, name="kp%d" % t) for t in range(PACK)]
         cp = [pool.tile([P, POS], F32, name="cp%d" % h) for h in range(2)]
         wp = [pool.tile([P, POS], F32, name="wp%d" % h) for h in range(2)]
-        q_raw = pool.tile([P, PACK, NQ], F32, name="q_raw", tag="q_raw", align_bytes=64)
+        q_raw = reused.tile([P, PACK, NQ], F32, name="q_raw", offset=0, align_bytes=64)
         kv = kT.rearrange("(p t) n -> p t n", t=PACK)
         cv = cT.rearrange("(p t) n -> p t n", t=PACK)
         wv = wT.rearrange("(p t) n -> p t n", t=PACK)
@@ -54,203 +57,155 @@ def tile_attend_pre_rope_f_topk_kernel(tc, qT, kT, cT, wT, offs, offs2, out):
         ident = pool.tile([P, P], F32, name="ident")
         make_identity(nc, ident[:])
 
-        cg = [pool.tile([P, N], F32, name="cg%d" % h) for h in range(2)]
-        wg = [pool.tile([P, N], F32, name="wg%d" % h) for h in range(2)]
-        wneg = [pool.tile([P, N], F32, name="wneg%d" % h) for h in range(2)]
-        kg = [pool.tile([P, N], F32, name="kg%d" % h) for h in range(2)]
-        kc = pool.tile([P, 2, N], F32, name="kc")
-        kw = pool.tile([P, 2, N], F32, name="kw")
-        first = pool.tile([P, 2, N], F32, name="first")
-        turned0 = pool.tile([P, N, 2], BF16, name="turned0")
-        turned0_words = turned0[:].rearrange("s n e -> s (n e)").bitcast(F32)
-        shared = pool.tile([P, 5 * P], F32, name="shared", align_bytes=64)
-        qb = shared[:, 0 : 4 * P].bitcast(BF16)
-        late_tiles = [pool.tile([P, 2, P], F32, name="late%d" % j) for j in range(3)]
-        late = [late_tiles[j][:] for j in range(3)] + [shared[:].rearrange("p (a b) -> p a b", b=P)[:, 0:5:4, :]]
-        u = [pool.tile([P, P, PACK], BF16, name="u%d" % j, tag="u%d" % j, align_bytes=64) for j in range(CHUNKS)]
-        u_words = [u[j][:].rearrange("p n t -> p (n t)").bitcast(F32).rearrange("p (n h) -> p n h", h=2) for j in range(CHUNKS)]
-        q_codes = pool.tile([P, NQ], U32, name="q_codes", align_bytes=64)
+        factors = [pool.tile([P, 3, N], F32, name="factors%d" % h) for h in range(2)]
+        kg1 = pool.tile([P, N], F32, name="kg1")
+        even = [pool.tile([P, 2, N], F32, name="even%d" % h) for h in range(2)]
+        odd0 = pool.tile([P, 2, N], F32, name="odd0")
+        turned0 = pool.tile([P, 2 * N], BF16, name="turned0")
+        qb = pool.tile([P, PACK * NQ], BF16, name="qb", align_bytes=64)
+        odd1 = pool.tile([P, 2, N], F32, name="odd1")
+        u = [pool.tile([P, w * PACK], BF16, name="u%d" % j, tag="u%d" % j, align_bytes=64) for j, w in enumerate((P, P, HALF))]
+        u_words = [tile[:].bitcast(F32).rearrange("p (n h) -> p n h", h=2) for tile in u]
+        q_codes = {}
         q_scales = pool.tile([P, NQ], U8, name="q_scales", align_bytes=64)
-        res = {}
         sums0 = [psum.tile([P, 2, 2 * P], F32, name="sums0%d" % g, tag="bank%d" % g) for g in range(2)]
-        back = [psum.tile([P, 2, P], F32, name="back%d" % j, tag="bank%d" % (5 + j)) for j in range(TURNED)]
-        back_rest = psum.tile([P, CHUNKS - TURNED, P], F32, name="back_rest", tag="bank4")
+        back = {j: psum.tile([P, 2, P], F32, name="back%d" % j) for j in TURNED}
+        back_added = psum.tile([P, 2, P], F32, name="back_added", tag="bank2")
         out_v = out[0].rearrange("(m p) n -> p m n", p=P)
 
-        def gather_table(dst, table):
-            nc.vector.tensor_copy(dst[:], table[:].indirect(pos[:]))
+        def slots(j):
+            return slice(j * P, (j + 1) * P)
 
-        def negate(h):
-            nc.scalar.activation(wneg[h][:], wg[h][:], COPY, scale=-1.0)
+        def gather_tables(h):
+            nc.vector.tensor_copy(factors[h][:, 2, :], wp[h][:].indirect(pos[:]))
+            nc.scalar.activation(factors[h][:, 0, :], factors[h][:, 2, :], COPY, scale=-1.0)
+            nc.vector.tensor_copy(factors[h][:, 1, :], cp[h][:].indirect(pos[:]))
 
-        def cos_product(t, lo, hi, dst):
-            nc.vector.tensor_tensor(dst, kp[t][:].indirect(tok[:, lo // 16 : hi // 16]), cg[t // 2][:, lo:hi], MULT)
-
-        def sin_product(t, lo, hi, dst):
-            w = wneg[t // 2] if t % 2 else wg[t // 2]
-            nc.vector.tensor_tensor(dst, kp[t][:].indirect(tok[:, lo // 16 : hi // 16]), w[:, lo:hi], MULT)
+        def fused_product(t, e, lo, hi, dst):
+            keys = kp[t][:].indirect(tok[:, lo // 16 : hi // 16])
+            nc.vector.tensor_tensor(dst, keys, factors[t // 2][:, 1 - t % 2 + e, lo:hi], MULT)
 
         def turn(dst, src, start, stop):
             nc.tensor.matmul(dst, src, ident[:], start=start, stop=stop, is_transpose=True)
 
-        def early_sum(src, t, start, stop):
-            for g in (1, 0):
-                for c in range(2):
-                    cols = slice((2 * g + c) * P, (2 * g + c + 1) * P)
-                    turn(sums0[g][:, t, c * P : (c + 1) * P], src[:, t, cols], start and c == 0, stop and c == 1)
+        def early_turn(src, e, start, stop):
+            for g, group in enumerate((ADDED, TURNED)):
+                for c, j in enumerate(group):
+                    turn(sums0[g][:, e, slots(c)], src[:, e, slots(j)], start and c == 0, stop and c == 1)
 
         def round_turned(dst, src):
             nc.scalar.copy(
-                dst.rearrange("s (c i) e -> s c e i", i=4),
+                dst.rearrange("s (c i e) -> s c e i", i=4, e=2),
                 src.rearrange("s e (c i) -> s c e i", i=4),
             )
 
-        def early_back(j):
-            dst = back[j][:, 0, :] if j < TURNED else back_rest[:, j - TURNED, :]
-            nc.tensor.transpose(dst, turned0_words[:, j * P : (j + 1) * P], ident[:])
-
         def add_late_pair(j):
-            cols = slice(j * P, (j + 1) * P)
             nc.vector.tensor_tensor(
-                u[j][:, :, 2:4].rearrange("p (c i) e -> p c e i", i=2),
-                first[:, :, cols].rearrange("p e (c i) -> p c e i", i=2),
-                late[j].rearrange("p e (c i) -> p c e i", i=2),
+                u[2][:].rearrange("p (n t) -> p n t", t=PACK)[:, slots(j - 2), 2:4].rearrange("p (c i) e -> p c e i", i=2),
+                even[1][:, :, slots(j)].rearrange("p e (c i) -> p c e i", i=2),
+                odd1[:, :, slots(j)].rearrange("p e (c i) -> p c e i", i=2),
                 ADD,
             )
 
         u_codes = {}
         u_scales = {}
 
-        def quantize(j, tag=None, scales=None):
-            codes = pool.tile([P, P], U32, name="u_codes%d" % j, tag=tag or "u_codes%d" % j, align_bytes=64)
-            u_codes[j] = codes[:]
-            if scales is None:
-                own = pool.tile([P, P], U8, name="u_scales%d" % j, align_bytes=64)
-                scales = own[:]
-            u_scales[j] = scales
-            nc.vector.quantize_mx(
-                out=u_codes[j].bitcast(FP8X4),
-                scales=u_scales[j],
-                in_=u[j][:].rearrange("p n t -> p (n t)"),
+        def quantize(j):
+            width = (P, P, HALF)[j]
+            u_codes[j] = reused.tile([P, width], U32, name="u_codes%d" % j, offset=(2560, 3072, 1280)[j], align_bytes=64)
+            u_scales[j] = pool.tile([P, width], U8, name="u_scales%d" % j, align_bytes=64)
+            nc.vector.quantize_mx(out=u_codes[j][:].bitcast(FP8X4), scales=u_scales[j][:], in_=u[j][:])
+
+        def score(j, m, acc):
+            nc.tensor.matmul_mx(
+                out=acc,
+                lhsT=q_codes[m][:].bitcast(FP8X4),
+                lhsT_scale=q_scales[:, slots(m)],
+                rhs=u_codes[j][:].bitcast(FP8X4),
+                rhs_scale=u_scales[j][:],
+                start=True,
+                stop=True,
             )
 
-        def quantize_queries(m):
-            rows = slice(m * P, (m + 1) * P)
-            nc.vector.quantize_mx(
-                out=q_codes[:, rows].bitcast(FP8X4), scales=q_scales[:, rows], in_=qb[:, m * PACK * P : (m + 1) * PACK * P]
-            )
-
-        def cast_queries():
-            nc.scalar.copy(
-                qb.rearrange("p (c i t) -> p c t i", i=2, t=PACK),
-                q_raw[:].rearrange("p t (c i) -> p c t i", i=2),
-            )
-
-        def scores(j, accs):
+        def finish(j, bank, copy, tag):
+            res = pool.tile([P, 2, P], F32, name="res%d" % j, tag=tag, align_bytes=64)
+            acc = psum.tile([P, 2, P], F32, name="acc%d" % j, tag=bank)
             for m in range(2):
-                rows = slice(m * P, (m + 1) * P)
-                nc.tensor.matmul_mx(
-                    out=accs[m],
-                    lhsT=q_codes[:, rows].bitcast(FP8X4),
-                    lhsT_scale=q_scales[:, rows],
-                    rhs=u_codes[j].bitcast(FP8X4),
-                    rhs_scale=u_scales[j],
-                    start=True,
-                    stop=True,
-                )
+                score(j, m, acc[:, m, :])
+            copy(res[:], acc[:])
+            nc.sync.dma_start(out=out_v[:, :, slots(j)], in_=res[:])
 
-        def finish(j, bank, engine_copy, tag):
-            res[j] = pool.tile([P, 2, P], F32, name="res%d" % j, tag=tag, align_bytes=64)
-            acc = psum.tile([P, 2, P], F32, name="acc%d" % j, tag="bank%d" % bank)
-            scores(j, [acc[:, 0, :], acc[:, 1, :]])
-            engine_copy(res[j][:], acc[:])
-            nc.sync.dma_start(out=out_v[:, :, j * P : (j + 1) * P], in_=res[j][:])
+        gather_tables(0)
+        nc.vector.tensor_copy(even[0][:, 0, :], kp[0][:].indirect(tok[:]))
+        nc.vector.tensor_tensor(even[0][:, 1, :], even[0][:, 0, :], factors[0][:, 2, :], MULT)
+        early_turn(even[0], 1, True, False)
+        nc.gpsimd.tensor_tensor(even[0][:, 0, :], even[0][:, 0, :], factors[0][:, 1, :], MULT)
+        early_turn(even[0], 0, False, False)
+        nc.vector.tensor_copy(kg1[:], kp[1][:].indirect(tok[:]))
+        for e in (1, 0):
+            nc.gpsimd.tensor_tensor(odd0[:, e, :], kg1[:], factors[0][:, e, :], MULT)
+            early_turn(odd0, e, False, e == 0)
+        turned0_words = turned0[:].bitcast(F32)
+        for g in range(2):
+            round_turned(turned0[:, g * N : (g + 1) * N], sums0[g][:])
+        for c in range(2):
+            nc.tensor.transpose(back_added[:, c, :], turned0_words[:, slots(c)], ident[:])
+        nc.scalar.copy(u_words[2][:, :, 0], back_added[:].rearrange("p c n -> p (c n)"))
+        for c, j in enumerate(TURNED):
+            nc.tensor.transpose(back[j][:, 0, :], turned0_words[:, slots(2 + c)], ident[:])
 
-        def finish_split(j, banks):
-            res[j] = pool.tile([P, 2, P], F32, name="res%d" % j)
-            accs = [psum.tile([P, P], F32, name="acc%d%d" % (j, m), tag="bank%d" % banks[m]) for m in range(2)]
-            scores(j, [accs[0][:], accs[1][:]])
-            nc.scalar.copy(res[j][:, 0, :], accs[0][:])
-            nc.vector.tensor_copy(res[j][:, 1, :], accs[1][:])
-            nc.sync.dma_start(out=out_v[:, :, j * P : (j + 1) * P], in_=res[j][:])
+        gather_tables(1)
+        fused_product(2, 0, 0, N, even[1][:, 0, :])
+        fused_product(2, 1, 0, N, even[1][:, 1, :])
+        sums1 = {}
+        for j, bank in zip(TURNED, ("bank2", "bank1")):
+            sums1[j] = psum.tile([P, 2, P], F32, name="sums1%d" % j, tag=bank)
+            turn(sums1[j][:, 0, :], even[1][:, 0, slots(j)], True, False)
+            turn(sums1[j][:, 1, :], even[1][:, 1, slots(j)], False, False)
 
-        def first_pair_sums():
-            for g in (1, 0):
-                round_turned(turned0[:, 2 * g * P : 2 * (g + 1) * P, :], sums0[g][:])
-            for j in range(TURNED, CHUNKS):
-                early_back(j)
-            for j in range(TURNED, CHUNKS):
-                nc.scalar.copy(u_words[j][:, :, 0], back_rest[:, j - TURNED, :])
-            for j in range(TURNED):
-                early_back(j)
+        nc.scalar.copy(
+            qb[:].rearrange("p (c i t) -> p c t i", i=4, t=PACK),
+            q_raw[:].rearrange("p t (c i) -> p c t i", i=4),
+        )
+        turned1 = reused.tile([P, 4 * P], BF16, name="turned1", offset=1024, align_bytes=64)
 
         last = PACK - 1
 
-        def late_cos(j):
-            cos_product(last, j * P, (j + 1) * P, late[j][:, 1, :])
-
-        def late_sin(j):
-            sin_product(last, j * P, (j + 1) * P, late[j][:, 0, :])
-
-        def late_sum(j):
-            turn(sums1[j][:, 1, :], late[j][:, 1, :], False, False)
-            turn(sums1[j][:, 0, :], late[j][:, 0, :], False, True)
-
-        def late_round(j):
-            round_turned(turned1[:, 2 * j * P : 2 * (j + 1) * P].rearrange("s (n e) -> s n e", e=2), sums1[j][:])
-
-        def late_back(j):
-            nc.tensor.transpose(back[j][:, 1, :], turned1[:, 2 * j * P : 2 * (j + 1) * P].bitcast(F32), ident[:])
+        for lo, hi in ((0, HALF), (HALF, HALF + P), (HALF + P, N)):
+            for e in (1, 0):
+                fused_product(last, e, lo, hi, odd1[:, e, lo:hi])
+        for j in TURNED:
+            turn(sums1[j][:, 1, :], odd1[:, 1, slots(j)], False, False)
+            turn(sums1[j][:, 0, :], odd1[:, 0, slots(j)], False, True)
+        for c, j in enumerate(TURNED):
+            round_turned(turned1[:, 2 * c * P : 2 * (c + 1) * P], sums1[j][:])
+        for c, j in enumerate(TURNED):
+            nc.tensor.transpose(back[j][:, 1, :], turned1[:, 2 * c * P : 2 * (c + 1) * P].bitcast(F32), ident[:])
             nc.scalar.copy(u_words[j], back[j][:].rearrange("p h n -> p n h"))
 
-        gather_table(wg[0], wp[0])
-        negate(0)
-        gather_table(cg[0], cp[0])
-        nc.vector.tensor_copy(kg[0][:], kp[0][:].indirect(tok[:]))
-        nc.vector.tensor_tensor(kw[:, 1, :], kg[0][:], wg[0][:], MULT)
-        early_sum(kw, 1, True, False)
-        nc.gpsimd.tensor_tensor(kc[:, 0, :], kg[0][:], cg[0][:], MULT)
-        early_sum(kc, 0, False, False)
-        nc.vector.tensor_copy(kg[1][:], kp[1][:].indirect(tok[:]))
-        nc.gpsimd.tensor_tensor(kc[:, 1, :], kg[1][:], cg[0][:], MULT)
-        early_sum(kc, 1, False, False)
-        nc.gpsimd.tensor_tensor(kw[:, 0, :], kg[1][:], wneg[0][:], MULT)
-        early_sum(kw, 0, False, True)
-        first_pair_sums()
-        gather_table(wg[1], wp[1])
-        negate(1)
-        gather_table(cg[1], cp[1])
-        sums1 = [psum.tile([P, 2, P], F32, name="sums1%d" % j, tag=("bank4", "bank0")[j]) for j in range(TURNED)]
-        cos_product(2, 0, N, first[:, 0, :])
-        sin_product(2, 0, N, first[:, 1, :])
-        for j in range(TURNED):
-            cols = slice(j * P, (j + 1) * P)
-            turn(sums1[j][:, 0, :], first[:, 0, cols], True, False)
-            turn(sums1[j][:, 1, :], first[:, 1, cols], False, False)
-        cast_queries()
-        turned1 = pool.tile([P, 2 * TURNED * P], BF16, name="turned1", tag="q_raw", align_bytes=64)
-        for j in range(TURNED):
-            late_cos(j)
-            late_sin(j)
-        late_sum(0)
-        late_sum(1)
-        late_round(0)
-        late_round(1)
-        late_back(0)
-        late_back(1)
-        late_cos(2)
-        late_sin(2)
-        late_cos(3)
+        def quantize_queries(m):
+            q_codes[m] = reused.tile([P, P], U32, name="q_codes%d" % m, offset=(0, 768)[m], align_bytes=64)
+            nc.vector.quantize_mx(
+                out=q_codes[m][:].bitcast(FP8X4), scales=q_scales[:, slots(m)], in_=qb[:, m * PACK * P : (m + 1) * PACK * P]
+            )
+
         add_late_pair(2)
-        quantize_queries(0)
-        quantize_queries(1)
-        late_sin(3)
-        quantize(2, scales=q_scales[4:P, 0:P])
-        finish(2, 0, nc.scalar.copy, "res2")
         add_late_pair(3)
+        quantize_queries(0)
+        quantize(2)
+        quantize_queries(1)
         quantize(0)
-        finish(0, 1, nc.scalar.copy, "res0")
-        quantize(3, "q_raw")
         quantize(1)
-        finish(3, 2, nc.vector.tensor_copy, "u1")
-        finish_split(1, (3, 7))
+        for m, bank, copy, tag in ((0, "bank1", nc.scalar.copy, "res20"), (1, "bank3", nc.vector.tensor_copy, "u1")):
+            acc = psum.tile([P, HALF], F32, name="acc2%d" % m, tag=bank)
+            score(2, m, acc[:])
+            res2 = pool.tile([P, HALF], F32, name="res2%d" % m, tag=tag, align_bytes=64)
+            copy(res2[:], acc[:])
+            nc.sync.dma_start(out=out_v[:, m, HALF:N], in_=res2[:])
+        finish(0, "bank0", nc.scalar.copy, "res0")
+        res1 = pool.tile([P, 2, P], F32, name="res1")
+        for m, bank in ((0, "bank4"), (1, "bank5")):
+            acc = psum.tile([P, P], F32, name="acc1%d" % m, tag=bank)
+            score(1, m, acc[:])
+            nc.vector.tensor_copy(res1[:, m, :], acc[:])
+        nc.sync.dma_start(out=out_v[:, :, slots(1)], in_=res1[:])

@@ -49,8 +49,8 @@ def tile_attend_pre_rope_f_topk_kernel(tc, qT, kT, cT, wT, offs, offs2, out):
         nc.sync.dma_start(out=kp[0][:], in_=kv[:, 0, :])
         nc.sync.dma_start(out=kp[1][:], in_=kv[:, 1, :])
         nc.sync.dma_start(out=wp[1][:], in_=wv[:, 2, :])
-        nc.sync.dma_start(out=cp[1][:], in_=cv[:, 2, :])
         nc.sync.dma_start(out=kp[2][:], in_=kv[:, 2, :])
+        nc.sync.dma_start(out=cp[1][:], in_=cv[:, 2, :])
         nc.sync.dma_start(out=kp[3][:], in_=kv[:, 3, :])
         nc.sync.dma_start(out=q_raw[:], in_=qT[0].rearrange("(p t) n -> p t n", t=PACK))
 
@@ -76,9 +76,11 @@ def tile_attend_pre_rope_f_topk_kernel(tc, qT, kT, cT, wT, offs, offs2, out):
         def slots(j):
             return slice(j * P, (j + 1) * P)
 
-        def gather_tables(h):
+        def gather_sines(h):
             nc.vector.tensor_copy(factors[h][:, 2, :], wp[h][:].indirect(pos[:]))
             nc.scalar.activation(factors[h][:, 0, :], factors[h][:, 2, :], COPY, scale=-1.0)
+
+        def gather_cosines(h):
             nc.vector.tensor_copy(factors[h][:, 1, :], cp[h][:].indirect(pos[:]))
 
         def fused_product(t, e, lo, hi, dst):
@@ -135,7 +137,8 @@ def tile_attend_pre_rope_f_topk_kernel(tc, qT, kT, cT, wT, offs, offs2, out):
             copy(res[:], acc[:])
             nc.sync.dma_start(out=out_v[:, :, slots(j)], in_=res[:])
 
-        gather_tables(0)
+        gather_sines(0)
+        gather_cosines(0)
         nc.vector.tensor_copy(even[0][:, 0, :], kp[0][:].indirect(tok[:]))
         nc.vector.tensor_tensor(even[0][:, 1, :], even[0][:, 0, :], factors[0][:, 2, :], MULT)
         early_turn(even[0], 1, True, False)
@@ -154,14 +157,17 @@ def tile_attend_pre_rope_f_topk_kernel(tc, qT, kT, cT, wT, offs, offs2, out):
         for c, j in enumerate(TURNED):
             nc.tensor.transpose(back[j][:, 0, :], turned0_words[:, slots(2 + c)], ident[:])
 
-        gather_tables(1)
-        fused_product(2, 0, 0, N, even[1][:, 0, :])
-        fused_product(2, 1, 0, N, even[1][:, 1, :])
+        gather_sines(1)
+        kg2 = pool.tile([P, N], F32, name="kg2")
+        nc.vector.tensor_copy(kg2[:], kp[2][:].indirect(tok[:]))
+        nc.gpsimd.tensor_tensor(even[1][:, 1, :], kg2[:], factors[1][:, 2, :], MULT)
+        gather_cosines(1)
+        nc.vector.tensor_tensor(even[1][:, 0, :], kg2[:], factors[1][:, 1, :], MULT)
         sums1 = {}
         for j, bank in zip(TURNED, ("bank2", "bank1")):
             sums1[j] = psum.tile([P, 2, P], F32, name="sums1%d" % j, tag=bank)
-            turn(sums1[j][:, 0, :], even[1][:, 0, slots(j)], True, False)
-            turn(sums1[j][:, 1, :], even[1][:, 1, slots(j)], False, False)
+            turn(sums1[j][:, 1, :], even[1][:, 1, slots(j)], True, False)
+            turn(sums1[j][:, 0, :], even[1][:, 0, slots(j)], False, False)
 
         nc.scalar.copy(
             qb[:].rearrange("p (c i t) -> p c t i", i=4, t=PACK),

@@ -58,15 +58,14 @@ def tile_attend_pre_rope_f_topk_kernel(tc, qT, kT, cT, wT, offs, offs2, out):
         make_identity(nc, ident[:])
 
         factors = [pool.tile([P, 3, N], F32, name="factors%d" % h) for h in range(2)]
-        kg1 = pool.tile([P, N], F32, name="kg1")
         even = [pool.tile([P, 2, N], F32, name="even%d" % h) for h in range(2)]
         odd0 = pool.tile([P, 2, N], F32, name="odd0")
         turned0 = pool.tile([P, 2 * N], BF16, name="turned0")
         qb = pool.tile([P, PACK * NQ], BF16, name="qb", align_bytes=64)
         odd1 = pool.tile([P, 2, N], F32, name="odd1")
-        u = [pool.tile([P, w * PACK], BF16, name="u%d" % j, tag="u%d" % j, align_bytes=64) for j, w in enumerate((P, P, HALF))]
+        u = [pool.tile([P, w * PACK], BF16, name="u%d" % j, tag="u%d" % j, align_bytes=64) for j, w in enumerate((P, P, P, P))]
         u_words = [tile[:].bitcast(F32).rearrange("p (n h) -> p n h", h=2) for tile in u]
-        q_codes = {}
+        q_codes = pool.tile([P, NQ], U32, name="q_codes", align_bytes=64)
         q_scales = pool.tile([P, NQ], U8, name="q_scales", align_bytes=64)
         sums0 = [psum.tile([P, 2, 2 * P], F32, name="sums0%d" % g, tag="bank%d" % g) for g in range(2)]
         back = {j: psum.tile([P, 2, P], F32, name="back%d" % j) for j in TURNED}
@@ -79,9 +78,6 @@ def tile_attend_pre_rope_f_topk_kernel(tc, qT, kT, cT, wT, offs, offs2, out):
         def gather_sines(h):
             nc.vector.tensor_copy(factors[h][:, 2, :], wp[h][:].indirect(pos[:]))
             nc.scalar.activation(factors[h][:, 0, :], factors[h][:, 2, :], COPY, scale=-1.0)
-
-        def gather_cosines(h):
-            nc.vector.tensor_copy(factors[h][:, 1, :], cp[h][:].indirect(pos[:]))
 
         def fused_product(t, e, lo, hi, dst):
             keys = kp[t][:].indirect(tok[:, lo // 16 : hi // 16])
@@ -103,7 +99,7 @@ def tile_attend_pre_rope_f_topk_kernel(tc, qT, kT, cT, wT, offs, offs2, out):
 
         def add_late_pair(j):
             nc.vector.tensor_tensor(
-                u[2][:].rearrange("p (n t) -> p n t", t=PACK)[:, slots(j - 2), 2:4].rearrange("p (c i) e -> p c e i", i=2),
+                u[j][:].rearrange("p (n t) -> p n t", t=PACK)[:, :, 2:4].rearrange("p (c i) e -> p c e i", i=2),
                 even[1][:, :, slots(j)].rearrange("p e (c i) -> p c e i", i=2),
                 odd1[:, :, slots(j)].rearrange("p e (c i) -> p c e i", i=2),
                 ADD,
@@ -113,15 +109,14 @@ def tile_attend_pre_rope_f_topk_kernel(tc, qT, kT, cT, wT, offs, offs2, out):
         u_scales = {}
 
         def quantize(j):
-            width = (P, P, HALF)[j]
-            u_codes[j] = reused.tile([P, width], U32, name="u_codes%d" % j, offset=(2560, 3072, 1280)[j], align_bytes=64)
-            u_scales[j] = pool.tile([P, width], U8, name="u_scales%d" % j, align_bytes=64)
+            u_codes[j] = reused.tile([P, P], U32, name="u_codes%d" % j, offset=(2560, 3072, 1024, 1536)[j], align_bytes=64)
+            u_scales[j] = pool.tile([P, P], U8, name="u_scales%d" % j, align_bytes=64)
             nc.vector.quantize_mx(out=u_codes[j][:].bitcast(FP8X4), scales=u_scales[j][:], in_=u[j][:])
 
         def score(j, m, acc):
             nc.tensor.matmul_mx(
                 out=acc,
-                lhsT=q_codes[m][:].bitcast(FP8X4),
+                lhsT=q_codes[:, slots(m)].bitcast(FP8X4),
                 lhsT_scale=q_scales[:, slots(m)],
                 rhs=u_codes[j][:].bitcast(FP8X4),
                 rhs_scale=u_scales[j][:],
@@ -138,33 +133,39 @@ def tile_attend_pre_rope_f_topk_kernel(tc, qT, kT, cT, wT, offs, offs2, out):
             nc.sync.dma_start(out=out_v[:, :, slots(j)], in_=res[:])
 
         gather_sines(0)
-        gather_cosines(0)
+        nc.vector.tensor_copy(factors[0][:, 1, :], cp[0][:].indirect(pos[:]))
         nc.vector.tensor_copy(even[0][:, 0, :], kp[0][:].indirect(tok[:]))
         nc.vector.tensor_tensor(even[0][:, 1, :], even[0][:, 0, :], factors[0][:, 2, :], MULT)
         early_turn(even[0], 1, True, False)
         nc.gpsimd.tensor_tensor(even[0][:, 0, :], even[0][:, 0, :], factors[0][:, 1, :], MULT)
         early_turn(even[0], 0, False, False)
-        nc.vector.tensor_copy(kg1[:], kp[1][:].indirect(tok[:]))
-        for e in (1, 0):
-            nc.gpsimd.tensor_tensor(odd0[:, e, :], kg1[:], factors[0][:, e, :], MULT)
-            early_turn(odd0, e, False, e == 0)
+        nc.vector.tensor_copy(odd0[:, 0, :], kp[1][:].indirect(tok[:]))
+        nc.vector.tensor_tensor(odd0[:, 1, :], odd0[:, 0, :], factors[0][:, 1, :], MULT)
+        early_turn(odd0, 1, False, False)
+        nc.gpsimd.tensor_tensor(odd0[:, 0, :], odd0[:, 0, :], factors[0][:, 0, :], MULT)
+        early_turn(odd0, 0, False, True)
         turned0_words = turned0[:].bitcast(F32)
         for g in range(2):
             round_turned(turned0[:, g * N : (g + 1) * N], sums0[g][:])
         for c in range(2):
             nc.tensor.transpose(back_added[:, c, :], turned0_words[:, slots(c)], ident[:])
-        nc.scalar.copy(u_words[2][:, :, 0], back_added[:].rearrange("p c n -> p (c n)"))
+        for c, j in enumerate(ADDED):
+            nc.scalar.copy(u_words[j], back_added[:, c, :].unsqueeze(2).to_broadcast([P, P, 2]))
         for c, j in enumerate(TURNED):
             nc.tensor.transpose(back[j][:, 0, :], turned0_words[:, slots(2 + c)], ident[:])
 
         gather_sines(1)
         kg2 = pool.tile([P, N], F32, name="kg2")
-        nc.vector.tensor_copy(kg2[:], kp[2][:].indirect(tok[:]))
-        nc.gpsimd.tensor_tensor(even[1][:, 1, :], kg2[:], factors[1][:, 2, :], MULT)
-        gather_cosines(1)
-        nc.vector.tensor_tensor(even[1][:, 0, :], kg2[:], factors[1][:, 1, :], MULT)
+        halves = (slice(0, HALF), slice(HALF, N))
+        for h, part in enumerate(halves):
+            nc.vector.tensor_copy(kg2[:, part], kp[2][:].indirect(tok[:, h * HALF // 16 : (h + 1) * HALF // 16]))
+            nc.gpsimd.tensor_tensor(even[1][:, 1, part], kg2[:, part], factors[1][:, 2, part], MULT)
+        for h, part in enumerate(halves):
+            nc.vector.tensor_copy(factors[1][:, 1, part], cp[1][:].indirect(pos[:, h * HALF // 16 : (h + 1) * HALF // 16]))
+        for part in halves:
+            nc.vector.tensor_tensor(even[1][:, 0, part], kg2[:, part], factors[1][:, 1, part], MULT)
         sums1 = {}
-        for j, bank in zip(TURNED, ("bank2", "bank1")):
+        for j, bank in zip(TURNED, ("bank0", "bank1")):
             sums1[j] = psum.tile([P, 2, P], F32, name="sums1%d" % j, tag=bank)
             turn(sums1[j][:, 1, :], even[1][:, 1, slots(j)], True, False)
             turn(sums1[j][:, 0, :], even[1][:, 0, slots(j)], False, False)
@@ -189,29 +190,17 @@ def tile_attend_pre_rope_f_topk_kernel(tc, qT, kT, cT, wT, offs, offs2, out):
             nc.tensor.transpose(back[j][:, 1, :], turned1[:, 2 * c * P : 2 * (c + 1) * P].bitcast(F32), ident[:])
             nc.scalar.copy(u_words[j], back[j][:].rearrange("p h n -> p n h"))
 
-        def quantize_queries(m):
-            q_codes[m] = reused.tile([P, P], U32, name="q_codes%d" % m, offset=(0, 768)[m], align_bytes=64)
-            nc.vector.quantize_mx(
-                out=q_codes[m][:].bitcast(FP8X4), scales=q_scales[:, slots(m)], in_=qb[:, m * PACK * P : (m + 1) * PACK * P]
-            )
-
         add_late_pair(2)
         add_late_pair(3)
-        quantize_queries(0)
-        quantize(2)
-        quantize_queries(1)
-        quantize(0)
-        quantize(1)
-        for m, bank, copy, tag in ((0, "bank1", nc.scalar.copy, "res20"), (1, "bank3", nc.vector.tensor_copy, "u1")):
-            acc = psum.tile([P, HALF], F32, name="acc2%d" % m, tag=bank)
-            score(2, m, acc[:])
-            res2 = pool.tile([P, HALF], F32, name="res2%d" % m, tag=tag, align_bytes=64)
-            copy(res2[:], acc[:])
-            nc.sync.dma_start(out=out_v[:, m, HALF:N], in_=res2[:])
-        finish(0, "bank0", nc.scalar.copy, "res0")
-        res1 = pool.tile([P, 2, P], F32, name="res1")
-        for m, bank in ((0, "bank4"), (1, "bank5")):
+        nc.vector.quantize_mx(out=q_codes[:].bitcast(FP8X4), scales=q_scales[:], in_=qb[:])
+        for j in ADDED + TURNED:
+            quantize(j)
+        finish(2, "bank3", nc.scalar.copy, "res2")
+        finish(3, "bank4", nc.scalar.copy, "res3")
+        finish(0, "bank2", nc.vector.tensor_copy, "u1")
+        for m, bank, copy in ((0, "bank5", nc.scalar.copy), (1, "bank0", nc.vector.tensor_copy)):
             acc = psum.tile([P, P], F32, name="acc1%d" % m, tag=bank)
             score(1, m, acc[:])
-            nc.vector.tensor_copy(res1[:, m, :], acc[:])
-        nc.sync.dma_start(out=out_v[:, :, slots(1)], in_=res1[:])
+            res1 = pool.tile([P, P], F32, name="res1%d" % m)
+            copy(res1[:], acc[:])
+            nc.sync.dma_start(out=out_v[:, m, slots(1)], in_=res1[:])

@@ -124,14 +124,6 @@ def tile_attend_pre_rope_f_topk_kernel(tc, qT, kT, cT, wT, offs, offs2, out):
                 stop=True,
             )
 
-        def finish(j, bank, copy, tag):
-            res = pool.tile([P, 2, P], F32, name="res%d" % j, tag=tag, align_bytes=64)
-            acc = psum.tile([P, 2, P], F32, name="acc%d" % j, tag=bank)
-            for m in range(2):
-                score(j, m, acc[:, m, :])
-            copy(res[:], acc[:])
-            nc.sync.dma_start(out=out_v[:, :, slots(j)], in_=res[:])
-
         gather_sines(0)
         nc.vector.tensor_copy(factors[0][:, 1, :], cp[0][:].indirect(pos[:]))
         nc.vector.tensor_copy(even[0][:, 0, :], kp[0][:].indirect(tok[:]))
@@ -195,12 +187,21 @@ def tile_attend_pre_rope_f_topk_kernel(tc, qT, kT, cT, wT, offs, offs2, out):
         nc.vector.quantize_mx(out=q_codes[:].bitcast(FP8X4), scales=q_scales[:], in_=qb[:])
         for j in ADDED + TURNED:
             quantize(j)
-        finish(2, "bank3", nc.scalar.copy, "res2")
-        finish(3, "bank4", nc.scalar.copy, "res3")
-        finish(0, "bank2", nc.vector.tensor_copy, "u1")
+        acc23 = [psum.tile([P, 2, P], F32, name="acc23%d" % m, tag=bank) for m, bank in enumerate(("bank3", "bank4"))]
+        for c, j in enumerate(ADDED):
+            for m in range(2):
+                score(j, m, acc23[m][:, c, :])
+        for m in range(2):
+            res23 = pool.tile([P, HALF], F32, name="res23%d" % m)
+            nc.scalar.copy(res23[:], acc23[m][:].rearrange("p c n -> p (c n)"))
+            nc.sync.dma_start(out=out_v[:, m, HALF:N], in_=res23[:])
+        res01 = pool.tile([P, 2, HALF], F32, name="res01", tag="u1", align_bytes=64)
+        acc0 = psum.tile([P, 2, P], F32, name="acc0", tag="bank2")
+        for m in range(2):
+            score(0, m, acc0[:, m, :])
+        nc.vector.tensor_copy(res01[:, :, slots(0)], acc0[:])
         for m, bank, copy in ((0, "bank5", nc.scalar.copy), (1, "bank0", nc.vector.tensor_copy)):
             acc = psum.tile([P, P], F32, name="acc1%d" % m, tag=bank)
             score(1, m, acc[:])
-            res1 = pool.tile([P, P], F32, name="res1%d" % m)
-            copy(res1[:], acc[:])
-            nc.sync.dma_start(out=out_v[:, m, slots(1)], in_=res1[:])
+            copy(res01[:, m, slots(1)], acc[:])
+            nc.sync.dma_start(out=out_v[:, m, 0:HALF], in_=res01[:, m, :])

@@ -29,7 +29,6 @@ def tile_attend_pre_rope_f_topk_kernel(tc, qT, kT, cT, wT, offs, offs2, out):
     nc = tc.nc
     with ExitStack() as ctx:
         pool = ctx.enter_context(tc.tile_pool(name="held", bufs=1))
-        reused = ctx.enter_context(tc.tile_pool(name="reused", bufs=1))
         psum = ctx.enter_context(tc.psum_pool(name="psum", bufs=1))
 
         tok = pool.tile([P, N // 16], U16, name="tok")
@@ -37,7 +36,8 @@ def tile_attend_pre_rope_f_topk_kernel(tc, qT, kT, cT, wT, offs, offs2, out):
         kp = [pool.tile([P, T], F32, name="kp%d" % t) for t in range(PACK)]
         cp = [pool.tile([P, POS], F32, name="cp%d" % h) for h in range(2)]
         wp = [pool.tile([P, POS], F32, name="wp%d" % h) for h in range(2)]
-        q_raw = reused.tile([P, PACK, NQ], F32, name="q_raw", offset=0, align_bytes=64)
+        q_row = pool.tile([P, PACK * NQ], F32, name="q_row", align_bytes=64)
+        q_raw = q_row[:].rearrange("p (t n) -> p t n", t=PACK)
         kv = kT.rearrange("(p t) n -> p t n", t=PACK)
         cv = cT.rearrange("(p t) n -> p t n", t=PACK)
         wv = wT.rearrange("(p t) n -> p t n", t=PACK)
@@ -52,7 +52,7 @@ def tile_attend_pre_rope_f_topk_kernel(tc, qT, kT, cT, wT, offs, offs2, out):
         nc.sync.dma_start(out=kp[2][:], in_=kv[:, 2, :])
         nc.sync.dma_start(out=cp[1][:], in_=cv[:, 2, :])
         nc.sync.dma_start(out=kp[3][:], in_=kv[:, 3, :])
-        nc.sync.dma_start(out=q_raw[:], in_=qT[0].rearrange("(p t) n -> p t n", t=PACK))
+        nc.sync.dma_start(out=q_raw, in_=qT[0].rearrange("(p t) n -> p t n", t=PACK))
 
         ident = pool.tile([P, P], F32, name="ident")
         make_identity(nc, ident[:])
@@ -61,12 +61,12 @@ def tile_attend_pre_rope_f_topk_kernel(tc, qT, kT, cT, wT, offs, offs2, out):
         even = [pool.tile([P, 2, N], F32, name="even%d" % h) for h in range(2)]
         odd0 = pool.tile([P, 2, N], F32, name="odd0")
         turned0 = pool.tile([P, 2 * N], BF16, name="turned0")
-        qb = pool.tile([P, PACK * NQ], BF16, name="qb", align_bytes=64)
+        qb = [pool.tile([P, PACK * P], BF16, name="qb%d" % m, align_bytes=64) for m in range(2)]
         odd1 = pool.tile([P, 2, N], F32, name="odd1")
         u = [pool.tile([P, w * PACK], BF16, name="u%d" % j, tag="u%d" % j, align_bytes=64) for j, w in enumerate((P, P, P, P))]
         u_words = [tile[:].bitcast(F32).rearrange("p (n h) -> p n h", h=2) for tile in u]
-        q_codes = pool.tile([P, NQ], U32, name="q_codes", align_bytes=64)
-        q_scales = pool.tile([P, NQ], U8, name="q_scales", align_bytes=64)
+        q_codes = [pool.tile([P, P], U32, name="q_codes%d" % m, align_bytes=64) for m in range(2)]
+        q_scales = [pool.tile([P, P], U8, name="q_scales%d" % m, align_bytes=64) for m in range(2)]
         sums0 = [psum.tile([P, 2, 2 * P], F32, name="sums0%d" % g, tag="bank%d" % g) for g in range(2)]
         back = {j: psum.tile([P, 2, P], F32, name="back%d" % j) for j in TURNED}
         back_added = psum.tile([P, 2, P], F32, name="back_added", tag="bank2")
@@ -109,15 +109,15 @@ def tile_attend_pre_rope_f_topk_kernel(tc, qT, kT, cT, wT, offs, offs2, out):
         u_scales = {}
 
         def quantize(j):
-            u_codes[j] = reused.tile([P, P], U32, name="u_codes%d" % j, offset=(2560, 3072, 1024, 1536)[j], align_bytes=64)
+            u_codes[j] = pool.tile([P, P], U32, name="u_codes%d" % j, align_bytes=64)
             u_scales[j] = pool.tile([P, P], U8, name="u_scales%d" % j, align_bytes=64)
             nc.vector.quantize_mx(out=u_codes[j][:].bitcast(FP8X4), scales=u_scales[j][:], in_=u[j][:])
 
         def score(j, m, acc):
             nc.tensor.matmul_mx(
                 out=acc,
-                lhsT=q_codes[:, slots(m)].bitcast(FP8X4),
-                lhsT_scale=q_scales[:, slots(m)],
+                lhsT=q_codes[m][:].bitcast(FP8X4),
+                lhsT_scale=q_scales[m][:],
                 rhs=u_codes[j][:].bitcast(FP8X4),
                 rhs_scale=u_scales[j][:],
                 start=True,
@@ -162,45 +162,55 @@ def tile_attend_pre_rope_f_topk_kernel(tc, qT, kT, cT, wT, offs, offs2, out):
             turn(sums1[j][:, 1, :], even[1][:, 1, slots(j)], True, False)
             turn(sums1[j][:, 0, :], even[1][:, 0, slots(j)], False, False)
 
-        nc.scalar.copy(
-            qb[:].rearrange("p (c i t) -> p c t i", i=4, t=PACK),
-            q_raw[:].rearrange("p t (c i) -> p c t i", i=4),
-        )
-        turned1 = reused.tile([P, 4 * P], BF16, name="turned1", offset=1024, align_bytes=64)
+        def cast_queries(lo, hi):
+            nc.scalar.copy(
+                qb[lo // P][:, lo % P * PACK : ((hi - 1) % P + 1) * PACK].rearrange("p (c i t) -> p c t i", i=4, t=PACK),
+                q_raw[:, :, lo:hi].rearrange("p t (c i) -> p c t i", i=4),
+            )
+
+        cast_queries(0, P)
+        turned1 = [q_row[:, c * NQ : c * NQ + P] for c in range(2)]
 
         last = PACK - 1
 
-        for lo, hi in ((0, HALF), (HALF, HALF + P), (HALF + P, N)):
+        for j in range(CHUNKS):
             for e in (1, 0):
-                fused_product(last, e, lo, hi, odd1[:, e, lo:hi])
+                fused_product(last, e, j * P, (j + 1) * P, odd1[:, e, slots(j)])
         for j in TURNED:
             turn(sums1[j][:, 1, :], odd1[:, 1, slots(j)], False, False)
             turn(sums1[j][:, 0, :], odd1[:, 0, slots(j)], False, True)
         for c, j in enumerate(TURNED):
-            round_turned(turned1[:, 2 * c * P : 2 * (c + 1) * P], sums1[j][:])
+            round_turned(turned1[c].bitcast(BF16), sums1[j][:])
+        cast_queries(P, P + P // 2)
+        cast_queries(P + P // 2, NQ)
         for c, j in enumerate(TURNED):
-            nc.tensor.transpose(back[j][:, 1, :], turned1[:, 2 * c * P : 2 * (c + 1) * P].bitcast(F32), ident[:])
+            nc.tensor.transpose(back[j][:, 1, :], turned1[c], ident[:])
             nc.scalar.copy(u_words[j], back[j][:].rearrange("p h n -> p n h"))
+
+        def quantize_queries(m):
+            nc.vector.quantize_mx(out=q_codes[m][:].bitcast(FP8X4), scales=q_scales[m][:], in_=qb[m][:])
 
         add_late_pair(2)
         add_late_pair(3)
-        nc.vector.quantize_mx(out=q_codes[:].bitcast(FP8X4), scales=q_scales[:], in_=qb[:])
-        for j in ADDED + TURNED:
-            quantize(j)
-        acc23 = [psum.tile([P, 2, P], F32, name="acc23%d" % m, tag=bank) for m, bank in enumerate(("bank3", "bank4"))]
-        for c, j in enumerate(ADDED):
-            for m in range(2):
-                score(j, m, acc23[m][:, c, :])
-        for m in range(2):
-            res23 = pool.tile([P, HALF], F32, name="res23%d" % m)
-            nc.scalar.copy(res23[:], acc23[m][:].rearrange("p c n -> p (c n)"))
+        quantize(2)
+        quantize_queries(0)
+        quantize(3)
+        quantize_queries(1)
+        quantize(0)
+        quantize(1)
+        for m, bank, copy, tag in ((0, "bank1", nc.scalar.copy, "res230"), (1, "bank0", nc.vector.tensor_copy, "u1")):
+            acc23 = psum.tile([P, 2, P], F32, name="acc23%d" % m, tag=bank)
+            for c, j in enumerate(ADDED):
+                score(j, m, acc23[:, c, :])
+            res23 = pool.tile([P, HALF], F32, name="res23%d" % m, tag=tag, align_bytes=64)
+            copy(res23[:], acc23[:].rearrange("p c n -> p (c n)"))
             nc.sync.dma_start(out=out_v[:, m, HALF:N], in_=res23[:])
-        res01 = pool.tile([P, 2, HALF], F32, name="res01", tag="u1", align_bytes=64)
+        res01 = pool.tile([P, 2, HALF], F32, name="res01")
         acc0 = psum.tile([P, 2, P], F32, name="acc0", tag="bank2")
         for m in range(2):
             score(0, m, acc0[:, m, :])
-        nc.vector.tensor_copy(res01[:, :, slots(0)], acc0[:])
-        for m, bank, copy in ((0, "bank5", nc.scalar.copy), (1, "bank0", nc.vector.tensor_copy)):
+        nc.scalar.copy(res01[:, :, slots(0)], acc0[:])
+        for m, bank, copy in ((0, "bank3", nc.vector.tensor_copy), (1, "bank4", nc.scalar.copy)):
             acc = psum.tile([P, P], F32, name="acc1%d" % m, tag=bank)
             score(1, m, acc[:])
             copy(res01[:, m, slots(1)], acc[:])

@@ -29,6 +29,7 @@ def tile_attend_pre_rope_f_topk_kernel(tc, qT, kT, cT, wT, offs, offs2, out):
     nc = tc.nc
     with ExitStack() as ctx:
         pool = ctx.enter_context(tc.tile_pool(name="held", bufs=1))
+        reused = ctx.enter_context(tc.tile_pool(name="reused", bufs=1))
         psum = ctx.enter_context(tc.psum_pool(name="psum", bufs=1))
 
         tok = pool.tile([P, N // 16], U16, name="tok")
@@ -36,7 +37,7 @@ def tile_attend_pre_rope_f_topk_kernel(tc, qT, kT, cT, wT, offs, offs2, out):
         kp = [pool.tile([P, T], F32, name="kp%d" % t) for t in range(PACK)]
         cp = [pool.tile([P, POS], F32, name="cp%d" % h) for h in range(2)]
         wp = [pool.tile([P, POS], F32, name="wp%d" % h) for h in range(2)]
-        q_row = pool.tile([P, PACK * NQ], F32, name="q_row", align_bytes=64)
+        q_row = reused.tile([P, PACK * NQ], F32, name="q_row", offset=0, align_bytes=64)
         q_raw = q_row[:].rearrange("p (t n) -> p t n", t=PACK)
         kv = kT.rearrange("(p t) n -> p t n", t=PACK)
         cv = cT.rearrange("(p t) n -> p t n", t=PACK)
@@ -65,10 +66,10 @@ def tile_attend_pre_rope_f_topk_kernel(tc, qT, kT, cT, wT, offs, offs2, out):
         odd1 = pool.tile([P, 2, N], F32, name="odd1")
         u = [pool.tile([P, w * PACK], BF16, name="u%d" % j, tag="u%d" % j, align_bytes=64) for j, w in enumerate((P, P, P, P))]
         u_words = [tile[:].bitcast(F32).rearrange("p (n h) -> p n h", h=2) for tile in u]
-        q_codes = [pool.tile([P, P], U32, name="q_codes%d" % m, align_bytes=64) for m in range(2)]
+        q_codes = {}
         q_scales = [pool.tile([P, P], U8, name="q_scales%d" % m, align_bytes=64) for m in range(2)]
         sums0 = [psum.tile([P, 2, 2 * P], F32, name="sums0%d" % g, tag="bank%d" % g) for g in range(2)]
-        back = {j: psum.tile([P, 2, P], F32, name="back%d" % j) for j in TURNED}
+        back = {j: psum.tile([P, 2, P], F32, name="back%d" % j, tag="back%d" % j) for j in TURNED}
         back_added = psum.tile([P, 2, P], F32, name="back_added", tag="bank2")
         out_v = out[0].rearrange("(m p) n -> p m n", p=P)
 
@@ -109,7 +110,7 @@ def tile_attend_pre_rope_f_topk_kernel(tc, qT, kT, cT, wT, offs, offs2, out):
         u_scales = {}
 
         def quantize(j):
-            u_codes[j] = pool.tile([P, P], U32, name="u_codes%d" % j, align_bytes=64)
+            u_codes[j] = reused.tile([P, P], U32, name="u_codes%d" % j, offset=512 * j, align_bytes=64)
             u_scales[j] = pool.tile([P, P], U8, name="u_scales%d" % j, align_bytes=64)
             nc.vector.quantize_mx(out=u_codes[j][:].bitcast(FP8X4), scales=u_scales[j][:], in_=u[j][:])
 
@@ -173,9 +174,11 @@ def tile_attend_pre_rope_f_topk_kernel(tc, qT, kT, cT, wT, offs, offs2, out):
 
         last = PACK - 1
 
-        for j in range(CHUNKS):
-            for e in (1, 0):
-                fused_product(last, e, j * P, (j + 1) * P, odd1[:, e, slots(j)])
+        for group in (TURNED, ADDED):
+            lo, hi = group[0] * P, (group[1] + 1) * P
+            fused_product(last, 1, lo, hi, odd1[:, 1, lo:hi])
+            for j in group:
+                fused_product(last, 0, j * P, (j + 1) * P, odd1[:, 0, slots(j)])
         for j in TURNED:
             turn(sums1[j][:, 1, :], odd1[:, 1, slots(j)], False, False)
             turn(sums1[j][:, 0, :], odd1[:, 0, slots(j)], False, True)
@@ -188,30 +191,24 @@ def tile_attend_pre_rope_f_topk_kernel(tc, qT, kT, cT, wT, offs, offs2, out):
             nc.scalar.copy(u_words[j], back[j][:].rearrange("p h n -> p n h"))
 
         def quantize_queries(m):
+            q_codes[m] = reused.tile([P, P], U32, name="q_codes%d" % m, offset=(4096, 2048)[m], align_bytes=64)
             nc.vector.quantize_mx(out=q_codes[m][:].bitcast(FP8X4), scales=q_scales[m][:], in_=qb[m][:])
 
         add_late_pair(2)
         add_late_pair(3)
-        quantize(2)
         quantize_queries(0)
+        quantize(2)
         quantize(3)
         quantize_queries(1)
         quantize(0)
         quantize(1)
-        for m, bank, copy, tag in ((0, "bank1", nc.scalar.copy, "res230"), (1, "bank0", nc.vector.tensor_copy, "u1")):
-            acc23 = psum.tile([P, 2, P], F32, name="acc23%d" % m, tag=bank)
-            for c, j in enumerate(ADDED):
-                score(j, m, acc23[:, c, :])
-            res23 = pool.tile([P, HALF], F32, name="res23%d" % m, tag=tag, align_bytes=64)
-            copy(res23[:], acc23[:].rearrange("p c n -> p (c n)"))
-            nc.sync.dma_start(out=out_v[:, m, HALF:N], in_=res23[:])
-        res01 = pool.tile([P, 2, HALF], F32, name="res01")
-        acc0 = psum.tile([P, 2, P], F32, name="acc0", tag="bank2")
-        for m in range(2):
-            score(0, m, acc0[:, m, :])
-        nc.scalar.copy(res01[:, :, slots(0)], acc0[:])
-        for m, bank, copy in ((0, "bank3", nc.vector.tensor_copy), (1, "bank4", nc.scalar.copy)):
-            acc = psum.tile([P, P], F32, name="acc1%d" % m, tag=bank)
-            score(1, m, acc[:])
-            copy(res01[:, m, slots(1)], acc[:])
-            nc.sync.dma_start(out=out_v[:, m, 0:HALF], in_=res01[:, m, :])
+        banks = ["bank3", "bank4", "bank5", "bank2", "bank0", "bank1", "back0", "back1"]
+        for group in (ADDED, TURNED):
+            for m, copy in enumerate((nc.scalar.copy, nc.vector.tensor_copy)):
+                tag = "u1" if (group, m) == (ADDED, 1) else "res%d%d" % (group[0], m)
+                res = pool.tile([P, HALF], F32, name="res%d%d" % (group[0], m), tag=tag, align_bytes=64)
+                for c, j in enumerate(group):
+                    acc = psum.tile([P, P], F32, name="acc%d%d" % (j, m), tag=banks.pop(0))
+                    score(j, m, acc[:])
+                    copy(res[:, slots(c)], acc[:])
+                nc.sync.dma_start(out=out_v[:, m, group[0] * P : group[0] * P + HALF], in_=res[:])

@@ -1,7 +1,6 @@
 from contextlib import ExitStack
 
 import concourse.mybir as mybir
-from concourse.masks import make_identity
 
 D, T, POS, N, NQ = 512, 2048, 1024, 512, 256
 FLOPS = 2 * D * N * NQ
@@ -21,194 +20,133 @@ P = 128
 PACK = 4
 CHUNKS = N // P
 HALF = N // 2
-TURNED = (0, 1)
-ADDED = (2, 3)
 
 
 def tile_attend_pre_rope_f_topk_kernel(tc, qT, kT, cT, wT, offs, offs2, out):
     nc = tc.nc
     with ExitStack() as ctx:
         pool = ctx.enter_context(tc.tile_pool(name="held", bufs=1))
-        reused = ctx.enter_context(tc.tile_pool(name="reused", bufs=1))
         psum = ctx.enter_context(tc.psum_pool(name="psum", bufs=1))
 
         tok = pool.tile([P, N // 16], U16, name="tok")
         pos = pool.tile([P, N // 16], U16, name="pos")
         kp = [pool.tile([P, T], F32, name="kp%d" % t) for t in range(PACK)]
-        cp = [pool.tile([P, POS], F32, name="cp%d" % h) for h in range(2)]
-        wp = [pool.tile([P, POS], F32, name="wp%d" % h) for h in range(2)]
-        q_row = reused.tile([P, PACK * NQ], F32, name="q_row", offset=0, align_bytes=64)
-        q_raw = q_row[:].rearrange("p (t n) -> p t n", t=PACK)
+        k3 = kp[3]
+        cos = [pool.tile([P, POS], F32, name="cos%d" % h) for h in range(2)]
+        sin = pool.tile([P, 2 * POS], F32, name="sin")
+        q_raw = pool.tile([P, PACK, NQ], F32, name="q_raw")
         kv = kT.rearrange("(p t) n -> p t n", t=PACK)
         cv = cT.rearrange("(p t) n -> p t n", t=PACK)
-        wv = wT.rearrange("(p t) n -> p t n", t=PACK)
+        wv = wT.rearrange("(p t) n -> p (t n)", t=PACK)
 
-        nc.sync.dma_start(out=wp[0][:], in_=wv[:, 0, :])
+        nc.sync.dma_start(out=sin[:], in_=wv[:, POS : 3 * POS])
         nc.sync.dma_start(pos[:], offs2)
-        nc.sync.dma_start(out=cp[0][:], in_=cv[:, 0, :])
+        nc.sync.dma_start(out=cos[0][:], in_=cv[:, 0, :])
         nc.sync.dma_start(tok[:], offs)
-        nc.sync.dma_start(out=kp[0][:], in_=kv[:, 0, :])
-        nc.sync.dma_start(out=kp[1][:], in_=kv[:, 1, :])
-        nc.sync.dma_start(out=wp[1][:], in_=wv[:, 2, :])
-        nc.sync.dma_start(out=kp[2][:], in_=kv[:, 2, :])
-        nc.sync.dma_start(out=cp[1][:], in_=cv[:, 2, :])
+        for t in range(3):
+            nc.sync.dma_start(out=kp[t][:], in_=kv[:, t, :])
+        nc.sync.dma_start(out=cos[1][:], in_=cv[:, 2, :])
         nc.sync.dma_start(out=kp[3][:], in_=kv[:, 3, :])
-        nc.sync.dma_start(out=q_raw, in_=qT[0].rearrange("(p t) n -> p t n", t=PACK))
+        nc.sync.dma_start(out=q_raw[:], in_=qT[0].rearrange("(p t) n -> p t n", t=PACK))
 
-        ident = pool.tile([P, P], F32, name="ident")
-        make_identity(nc, ident[:])
-
-        factors = [pool.tile([P, 3, N], F32, name="factors%d" % h) for h in range(2)]
-        even = [pool.tile([P, 2, N], F32, name="even%d" % h) for h in range(2)]
+        kg = [pool.tile([P, N], F32, name="kg%d" % t) for t in range(3)]
+        factors0 = pool.tile([P, 3, N], F32, name="factors0")
+        even0 = pool.tile([P, 2, N], F32, name="even0")
         odd0 = pool.tile([P, 2, N], F32, name="odd0")
-        turned0 = pool.tile([P, 2 * N], BF16, name="turned0")
-        qb = [pool.tile([P, PACK * P], BF16, name="qb%d" % m, align_bytes=64) for m in range(2)]
-        odd1 = pool.tile([P, 2, N], F32, name="odd1")
-        u = [pool.tile([P, w * PACK], BF16, name="u%d" % j, tag="u%d" % j, align_bytes=64) for j, w in enumerate((P, P, P, P))]
-        u_words = [tile[:].bitcast(F32).rearrange("p (n h) -> p n h", h=2) for tile in u]
-        q_codes = {}
+        late = (slice(0, P), slice(P, HALF), slice(HALF, N))
+        kg3 = [pool.tile([P, part.stop - part.start], F32, name="kg3%d" % i) for i, part in enumerate(late)]
+        factors = pool.tile([P, 3, N], F32, name="factors")
+        even = pool.tile([P, 2, N], F32, name="even")
+        odd = [pool.tile([P, 2, HALF], F32, name="odd%d" % g) for g in range(2)]
+        groups = (slice(0, HALF), slice(HALF, HALF + P), slice(HALF + P, N))
+        widths = [part.stop - part.start for part in groups]
+        u = [pool.tile([P, w * PACK], BF16, name="u%d" % j, align_bytes=64) for j, w in enumerate(widths)]
+        qb = [pool.tile([P, P * PACK], BF16, name="qb%d" % m, align_bytes=64) for m in range(2)]
+        u_codes = [pool.tile([P, w], U32, name="u_codes%d" % j, align_bytes=64) for j, w in enumerate(widths)]
+        u_scales = [pool.tile([P, w], U8, name="u_scales%d" % j, align_bytes=64) for j, w in enumerate(widths)]
+        q_codes = [pool.tile([P, P], U32, name="q_codes%d" % m, align_bytes=64) for m in range(2)]
         q_scales = [pool.tile([P, P], U8, name="q_scales%d" % m, align_bytes=64) for m in range(2)]
-        sums0 = [psum.tile([P, 2, 2 * P], F32, name="sums0%d" % g, tag="bank%d" % g) for g in range(2)]
-        back = {j: psum.tile([P, 2, P], F32, name="back%d" % j, tag="back%d" % j) for j in TURNED}
-        back_added = psum.tile([P, 2, P], F32, name="back_added", tag="bank2")
         out_v = out[0].rearrange("(m p) n -> p m n", p=P)
 
         def slots(j):
             return slice(j * P, (j + 1) * P)
 
-        def gather_sines(h):
-            nc.vector.tensor_copy(factors[h][:, 2, :], wp[h][:].indirect(pos[:]))
-            nc.scalar.activation(factors[h][:, 0, :], factors[h][:, 2, :], COPY, scale=-1.0)
+        def listed(window, offsets, part):
+            return window.indirect(offsets[:, part.start // 16 : part.stop // 16])
 
-        def fused_product(t, e, lo, hi, dst):
-            keys = kp[t][:].indirect(tok[:, lo // 16 : hi // 16])
-            nc.vector.tensor_tensor(dst, keys, factors[t // 2][:, 1 - t % 2 + e, lo:hi], MULT)
+        def scalar_gather(dst, window, offsets, part):
+            nc.scalar.activation(dst, listed(window, offsets, part), COPY)
 
-        def turn(dst, src, start, stop):
-            nc.tensor.matmul(dst, src, ident[:], start=start, stop=stop, is_transpose=True)
+        def twice(src, width):
+            return src.unsqueeze(1).to_broadcast([P, 2, width])
 
-        def early_turn(src, e, start, stop):
-            for g, group in enumerate((ADDED, TURNED)):
-                for c, j in enumerate(group):
-                    turn(sums0[g][:, e, slots(c)], src[:, e, slots(j)], start and c == 0, stop and c == 1)
-
-        def round_turned(dst, src):
-            nc.scalar.copy(
-                dst.rearrange("s (c i e) -> s c e i", i=4, e=2),
-                src.rearrange("s e (c i) -> s c e i", i=4),
-            )
-
-        def add_late_pair(j):
+        def add_pair(j, h, a, b):
             nc.vector.tensor_tensor(
-                u[j][:].rearrange("p (n t) -> p n t", t=PACK)[:, :, 2:4].rearrange("p (c i) e -> p c e i", i=2),
-                even[1][:, :, slots(j)].rearrange("p e (c i) -> p c e i", i=2),
-                odd1[:, :, slots(j)].rearrange("p e (c i) -> p c e i", i=2),
+                u[j][:].rearrange("p (n t) -> p n t", t=PACK)[:, :, 2 * h : 2 * h + 2].rearrange("p (c i) e -> p c e i", i=2),
+                a.rearrange("p e (c i) -> p c e i", i=2),
+                b.rearrange("p e (c i) -> p c e i", i=2),
                 ADD,
             )
 
-        u_codes = {}
-        u_scales = {}
+        def quantize(codes, scales, src):
+            nc.vector.quantize_mx(out=codes[:].bitcast(FP8X4), scales=scales[:], in_=src[:])
 
-        def quantize(j):
-            u_codes[j] = reused.tile([P, P], U32, name="u_codes%d" % j, offset=512 * j, align_bytes=64)
-            u_scales[j] = pool.tile([P, P], U8, name="u_scales%d" % j, align_bytes=64)
-            nc.vector.quantize_mx(out=u_codes[j][:].bitcast(FP8X4), scales=u_scales[j][:], in_=u[j][:])
-
-        def score(j, m, acc):
-            nc.tensor.matmul_mx(
-                out=acc,
-                lhsT=q_codes[m][:].bitcast(FP8X4),
-                lhsT_scale=q_scales[m][:],
-                rhs=u_codes[j][:].bitcast(FP8X4),
-                rhs_scale=u_scales[j][:],
-                start=True,
-                stop=True,
-            )
-
-        gather_sines(0)
-        nc.vector.tensor_copy(factors[0][:, 1, :], cp[0][:].indirect(pos[:]))
-        nc.vector.tensor_copy(even[0][:, 0, :], kp[0][:].indirect(tok[:]))
-        nc.vector.tensor_tensor(even[0][:, 1, :], even[0][:, 0, :], factors[0][:, 2, :], MULT)
-        early_turn(even[0], 1, True, False)
-        nc.gpsimd.tensor_tensor(even[0][:, 0, :], even[0][:, 0, :], factors[0][:, 1, :], MULT)
-        early_turn(even[0], 0, False, False)
-        nc.vector.tensor_copy(odd0[:, 0, :], kp[1][:].indirect(tok[:]))
-        nc.vector.tensor_tensor(odd0[:, 1, :], odd0[:, 0, :], factors[0][:, 1, :], MULT)
-        early_turn(odd0, 1, False, False)
-        nc.gpsimd.tensor_tensor(odd0[:, 0, :], odd0[:, 0, :], factors[0][:, 0, :], MULT)
-        early_turn(odd0, 0, False, True)
-        turned0_words = turned0[:].bitcast(F32)
-        for g in range(2):
-            round_turned(turned0[:, g * N : (g + 1) * N], sums0[g][:])
-        for c in range(2):
-            nc.tensor.transpose(back_added[:, c, :], turned0_words[:, slots(c)], ident[:])
-        for c, j in enumerate(ADDED):
-            nc.scalar.copy(u_words[j], back_added[:, c, :].unsqueeze(2).to_broadcast([P, P, 2]))
-        for c, j in enumerate(TURNED):
-            nc.tensor.transpose(back[j][:, 0, :], turned0_words[:, slots(2 + c)], ident[:])
-
-        gather_sines(1)
-        kg2 = pool.tile([P, N], F32, name="kg2")
+        every = slice(0, N)
         halves = (slice(0, HALF), slice(HALF, N))
-        for h, part in enumerate(halves):
-            nc.vector.tensor_copy(kg2[:, part], kp[2][:].indirect(tok[:, h * HALF // 16 : (h + 1) * HALF // 16]))
-            nc.gpsimd.tensor_tensor(even[1][:, 1, part], kg2[:, part], factors[1][:, 2, part], MULT)
-        for h, part in enumerate(halves):
-            nc.vector.tensor_copy(factors[1][:, 1, part], cp[1][:].indirect(pos[:, h * HALF // 16 : (h + 1) * HALF // 16]))
+
+        for h, dst in enumerate((factors0, factors)):
+            nc.vector.tensor_copy(dst[:, 2, :], listed(sin[:, h * POS : (h + 1) * POS], pos, every))
+            nc.scalar.activation(dst[:, 0, :], dst[:, 2, :], COPY, scale=-1.0)
+        nc.vector.tensor_copy(factors0[:, 1, :], listed(cos[0][:], pos, every))
+        for t, dst in enumerate((even0, odd0)):
+            for part in halves:
+                scalar_gather(kg[t][:, part], kp[t][:], tok, part)
+                nc.vector.tensor_tensor(dst[:, :, part], twice(kg[t][:, part], HALF), factors0[:, 1 - t : 3 - t, part], MULT)
+        for j, part in enumerate(groups):
+            add_pair(j, 0, even0[:, :, part], odd0[:, :, part])
+        scalar_gather(kg[2][:], kp[2][:], tok, every)
+        nc.vector.tensor_tensor(even[:, 1, :], kg[2][:], factors[:, 2, :], MULT)
         for part in halves:
-            nc.vector.tensor_tensor(even[1][:, 0, part], kg2[:, part], factors[1][:, 1, part], MULT)
-        sums1 = {}
-        for j, bank in zip(TURNED, ("bank0", "bank1")):
-            sums1[j] = psum.tile([P, 2, P], F32, name="sums1%d" % j, tag=bank)
-            turn(sums1[j][:, 1, :], even[1][:, 1, slots(j)], True, False)
-            turn(sums1[j][:, 0, :], even[1][:, 0, slots(j)], False, False)
+            scalar_gather(factors[:, 1, part], cos[1][:], pos, part)
+            nc.vector.tensor_tensor(even[:, 0, part], kg[2][:, part], factors[:, 1, part], MULT)
 
-        def cast_queries(lo, hi):
+        scalar_gather(kg3[0][:], k3[:], tok, late[0])
+        nc.vector.tensor_copy(kg3[1][:], listed(k3[:], tok, late[1]))
+        scalar_gather(kg3[2][:], k3[:], tok, late[2])
+        for m in range(2):
             nc.scalar.copy(
-                qb[lo // P][:, lo % P * PACK : ((hi - 1) % P + 1) * PACK].rearrange("p (c i t) -> p c t i", i=4, t=PACK),
-                q_raw[:, :, lo:hi].rearrange("p t (c i) -> p c t i", i=4),
+                qb[m][:].rearrange("p (c i t) -> p c t i", i=4, t=PACK),
+                q_raw[:, :, slots(m)].rearrange("p t (c i) -> p c t i", i=4),
             )
+        for i, part in enumerate(late):
+            width = part.stop - part.start
+            lo = part.start % HALF
+            nc.vector.tensor_tensor(odd[part.start // HALF][:, :, lo : lo + width], twice(kg3[i][:], width), factors[:, 0:2, part], MULT)
+        add_pair(0, 1, even[:, :, groups[0]], odd[0][:])
+        quantize(q_codes[0], q_scales[0], qb[0])
+        quantize(u_codes[0], u_scales[0], u[0])
+        add_pair(1, 1, even[:, :, groups[1]], odd[1][:, :, 0:P])
+        quantize(q_codes[1], q_scales[1], qb[1])
+        add_pair(2, 1, even[:, :, groups[2]], odd[1][:, :, P:HALF])
+        quantize(u_codes[1], u_scales[1], u[1])
+        quantize(u_codes[2], u_scales[2], u[2])
 
-        cast_queries(0, P)
-        turned1 = [q_row[:, c * NQ : c * NQ + P] for c in range(2)]
-
-        last = PACK - 1
-
-        for group in (TURNED, ADDED):
-            lo, hi = group[0] * P, (group[1] + 1) * P
-            fused_product(last, 1, lo, hi, odd1[:, 1, lo:hi])
-            for j in group:
-                fused_product(last, 0, j * P, (j + 1) * P, odd1[:, 0, slots(j)])
-        for j in TURNED:
-            turn(sums1[j][:, 1, :], odd1[:, 1, slots(j)], False, False)
-            turn(sums1[j][:, 0, :], odd1[:, 0, slots(j)], False, True)
-        for c, j in enumerate(TURNED):
-            round_turned(turned1[c].bitcast(BF16), sums1[j][:])
-        cast_queries(P, P + P // 2)
-        cast_queries(P + P // 2, NQ)
-        for c, j in enumerate(TURNED):
-            nc.tensor.transpose(back[j][:, 1, :], turned1[c], ident[:])
-            nc.scalar.copy(u_words[j], back[j][:].rearrange("p h n -> p n h"))
-
-        def quantize_queries(m):
-            q_codes[m] = reused.tile([P, P], U32, name="q_codes%d" % m, offset=(4096, 2048)[m], align_bytes=64)
-            nc.vector.quantize_mx(out=q_codes[m][:].bitcast(FP8X4), scales=q_scales[m][:], in_=qb[m][:])
-
-        add_late_pair(2)
-        add_late_pair(3)
-        quantize_queries(0)
-        quantize(2)
-        quantize(3)
-        quantize_queries(1)
-        quantize(0)
-        quantize(1)
-        banks = ["bank3", "bank4", "bank5", "bank2", "bank0", "bank1", "back0", "back1"]
-        for group in (ADDED, TURNED):
-            for m, copy in enumerate((nc.scalar.copy, nc.vector.tensor_copy)):
-                tag = "u1" if (group, m) == (ADDED, 1) else "res%d%d" % (group[0], m)
-                res = pool.tile([P, HALF], F32, name="res%d%d" % (group[0], m), tag=tag, align_bytes=64)
-                for c, j in enumerate(group):
-                    acc = psum.tile([P, P], F32, name="acc%d%d" % (j, m), tag=banks.pop(0))
-                    score(j, m, acc[:])
-                    copy(res[:, slots(c)], acc[:])
-                nc.sync.dma_start(out=out_v[:, m, group[0] * P : group[0] * P + HALF], in_=res[:])
+        res = {(g, m): pool.tile([P, HALF], F32, name="res%d%d" % (g, m)) for g in range(2) for m in range(2)}
+        for j, part in enumerate(groups):
+            g = part.start // HALF
+            lo = part.start % HALF
+            for m in range(2):
+                acc = psum.tile([P, widths[j]], F32, name="acc%d%d" % (j, m))
+                nc.tensor.matmul_mx(
+                    out=acc[:],
+                    lhsT=q_codes[m][:].bitcast(FP8X4),
+                    lhsT_scale=q_scales[m][:],
+                    rhs=u_codes[j][:].bitcast(FP8X4),
+                    rhs_scale=u_scales[j][:],
+                    start=True,
+                    stop=True,
+                )
+                copy = nc.vector.tensor_copy if (j, m) == (2, 1) else nc.scalar.copy
+                copy(res[g, m][:, lo : lo + widths[j]], acc[:])
+                if part.stop % HALF == 0:
+                    nc.sync.dma_start(out=out_v[:, m, halves[g]], in_=res[g, m][:])

@@ -30,34 +30,37 @@ def tile_attend_pre_rope_f_topk_kernel(tc, qT, kT, cT, wT, offs, offs2, out):
 
         tok = pool.tile([P, N // 16], U16, name="tok")
         pos = pool.tile([P, N // 16], U16, name="pos")
-        kp = [pool.tile([P, T], F32, name="kp%d" % t) for t in range(PACK)]
-        k3 = kp[3]
+        k01 = pool.tile([P, 2 * T], F32, name="k01")
+        k2 = pool.tile([P, T], F32, name="k2")
+        k3 = pool.tile([P, T], F32, name="k3")
         cos = [pool.tile([P, POS], F32, name="cos%d" % h) for h in range(2)]
         sin = pool.tile([P, 2 * POS], F32, name="sin")
         q_raw = pool.tile([P, PACK, NQ], F32, name="q_raw")
-        kv = kT.rearrange("(p t) n -> p t n", t=PACK)
+        kv = kT.rearrange("(p t) n -> p (t n)", t=PACK)
         cv = cT.rearrange("(p t) n -> p t n", t=PACK)
         wv = wT.rearrange("(p t) n -> p (t n)", t=PACK)
 
         nc.sync.dma_start(out=sin[:], in_=wv[:, POS : 3 * POS])
         nc.sync.dma_start(pos[:], offs2)
-        nc.sync.dma_start(out=cos[0][:], in_=cv[:, 0, :])
         nc.sync.dma_start(tok[:], offs)
-        for t in range(3):
-            nc.sync.dma_start(out=kp[t][:], in_=kv[:, t, :])
+        nc.sync.dma_start(out=k01[:], in_=kv[:, 0 : 2 * T])
+        nc.sync.dma_start(out=cos[0][:], in_=cv[:, 0, :])
+        nc.sync.dma_start(out=k2[:], in_=kv[:, 2 * T : 3 * T])
         nc.sync.dma_start(out=cos[1][:], in_=cv[:, 2, :])
-        nc.sync.dma_start(out=kp[3][:], in_=kv[:, 3, :])
+        nc.sync.dma_start(out=k3[:], in_=kv[:, 3 * T : 4 * T])
         nc.sync.dma_start(out=q_raw[:], in_=qT[0].rearrange("(p t) n -> p t n", t=PACK))
 
-        kg = [pool.tile([P, N], F32, name="kg%d" % t) for t in range(3)]
-        factors0 = pool.tile([P, 3, N], F32, name="factors0")
-        even0 = pool.tile([P, 2, N], F32, name="even0")
-        odd0 = pool.tile([P, 2, N], F32, name="odd0")
+        kg01 = pool.tile([P, 2, N], F32, name="kg01")
+        kg2 = pool.tile([P, N], F32, name="kg2")
+        sin0 = pool.tile([P, N], F32, name="sin0")
+        cos0_listed = [pool.tile([P, HALF], F32, name="cos0_listed%d" % g) for g in range(2)]
+        by_sin = pool.tile([P, 2, N], F32, name="by_sin")
+        by_cos = [pool.tile([P, 2, HALF], F32, name="by_cos%d" % g) for g in range(2)]
         late = (slice(0, P), slice(P, HALF), slice(HALF, N))
-        kg3 = [pool.tile([P, part.stop - part.start], F32, name="kg3%d" % i) for i, part in enumerate(late)]
+        kg3 = {i: pool.tile([P, late[i].stop - late[i].start], F32, name="kg3%d" % i) for i in (1, 2)}
         factors = pool.tile([P, 3, N], F32, name="factors")
         even = pool.tile([P, 2, N], F32, name="even")
-        odd = [pool.tile([P, 2, HALF], F32, name="odd%d" % g) for g in range(2)]
+        odd = [pool.tile([P, 2, part.stop - part.start], F32, name="odd%d" % i) for i, part in enumerate(late)]
         groups = (slice(0, HALF), slice(HALF, HALF + P), slice(HALF + P, N))
         widths = [part.stop - part.start for part in groups]
         u = [pool.tile([P, w * PACK], BF16, name="u%d" % j, align_bytes=64) for j, w in enumerate(widths)]
@@ -80,9 +83,9 @@ def tile_attend_pre_rope_f_topk_kernel(tc, qT, kT, cT, wT, offs, offs2, out):
         def twice(src, width):
             return src.unsqueeze(1).to_broadcast([P, 2, width])
 
-        def add_pair(j, h, a, b):
+        def add_pair(dst, h, a, b):
             nc.vector.tensor_tensor(
-                u[j][:].rearrange("p (n t) -> p n t", t=PACK)[:, :, 2 * h : 2 * h + 2].rearrange("p (c i) e -> p c e i", i=2),
+                dst.rearrange("p (n t) -> p n t", t=PACK)[:, :, 2 * h : 2 * h + 2].rearrange("p (c i) e -> p c e i", i=2),
                 a.rearrange("p e (c i) -> p c e i", i=2),
                 b.rearrange("p e (c i) -> p c e i", i=2),
                 ADD,
@@ -94,40 +97,52 @@ def tile_attend_pre_rope_f_topk_kernel(tc, qT, kT, cT, wT, offs, offs2, out):
         every = slice(0, N)
         halves = (slice(0, HALF), slice(HALF, N))
 
-        for h, dst in enumerate((factors0, factors)):
-            nc.vector.tensor_copy(dst[:, 2, :], listed(sin[:, h * POS : (h + 1) * POS], pos, every))
-            nc.scalar.activation(dst[:, 0, :], dst[:, 2, :], COPY, scale=-1.0)
-        nc.vector.tensor_copy(factors0[:, 1, :], listed(cos[0][:], pos, every))
-        for t, dst in enumerate((even0, odd0)):
-            for part in halves:
-                scalar_gather(kg[t][:, part], kp[t][:], tok, part)
-                nc.vector.tensor_tensor(dst[:, :, part], twice(kg[t][:, part], HALF), factors0[:, 1 - t : 3 - t, part], MULT)
+        nc.vector.tensor_copy(factors[:, 2, :], listed(sin[:, POS : 2 * POS], pos, every))
+        nc.scalar.activation(factors[:, 0, :], factors[:, 2, :], COPY, scale=-1.0)
+        nc.vector.tensor_copy(sin0[:], listed(sin[:, 0:POS], pos, every))
+        nc.vector.tensor_copy(kg01[:, 0, :], listed(k01[:, 0:T], tok, every))
+        scalar_gather(kg01[:, 1, :], k01[:, T : 2 * T], tok, every)
+        for g, part in enumerate(halves):
+            scalar_gather(cos0_listed[g][:], cos[0][:], pos, part)
+        nc.vector.scalar_tensor_tensor(by_sin[:, 0, :], kg01[:, 1, :], -1.0, sin0[:], MULT, MULT)
+        nc.vector.tensor_tensor(by_sin[:, 1, :], kg01[:, 0, :], sin0[:], MULT)
+        for g, part in enumerate(halves):
+            nc.vector.tensor_tensor(by_cos[g][:], kg01[:, :, part], twice(cos0_listed[g][:], HALF), MULT)
         for j, part in enumerate(groups):
-            add_pair(j, 0, even0[:, :, part], odd0[:, :, part])
-        scalar_gather(kg[2][:], kp[2][:], tok, every)
-        nc.vector.tensor_tensor(even[:, 1, :], kg[2][:], factors[:, 2, :], MULT)
+            lo = part.start % HALF
+            add_pair(u[j][:], 0, by_cos[part.start // HALF][:, :, lo : lo + widths[j]], by_sin[:, :, part])
+        scalar_gather(kg2[:], k2[:], tok, every)
+        nc.vector.tensor_tensor(even[:, 1, :], kg2[:], factors[:, 2, :], MULT)
         for part in halves:
             scalar_gather(factors[:, 1, part], cos[1][:], pos, part)
-            nc.vector.tensor_tensor(even[:, 0, part], kg[2][:, part], factors[:, 1, part], MULT)
+            nc.vector.tensor_tensor(even[:, 0, part], kg2[:, part], factors[:, 1, part], MULT)
 
-        scalar_gather(kg3[0][:], k3[:], tok, late[0])
-        nc.vector.tensor_copy(kg3[1][:], listed(k3[:], tok, late[1]))
-        scalar_gather(kg3[2][:], k3[:], tok, late[2])
+        for i in (1, 2):
+            scalar_gather(kg3[i][:], k3[:], tok, late[i])
         for m in range(2):
             nc.scalar.copy(
                 qb[m][:].rearrange("p (c i t) -> p c t i", i=4, t=PACK),
                 q_raw[:, :, slots(m)].rearrange("p t (c i) -> p c t i", i=4),
             )
-        for i, part in enumerate(late):
-            width = part.stop - part.start
-            lo = part.start % HALF
-            nc.vector.tensor_tensor(odd[part.start // HALF][:, :, lo : lo + width], twice(kg3[i][:], width), factors[:, 0:2, part], MULT)
-        add_pair(0, 1, even[:, :, groups[0]], odd[0][:])
+
+        def late_product(i):
+            width = late[i].stop - late[i].start
+            nc.vector.tensor_tensor(odd[i][:], twice(kg3[i][:], width), factors[:, 0:2, late[i]], MULT)
+
+        def late_add(j, dst, src):
+            add_pair(dst, 1, even[:, :, slots(j)], src)
+
+        for e in range(2):
+            nc.vector.tensor_tensor(odd[0][:, e, :], listed(k3[:], tok, late[0]), factors[:, e, late[0]], MULT)
+        late_product(1)
+        late_add(0, u[0][:, 0 : PACK * P], odd[0][:])
+        late_product(2)
+        late_add(1, u[0][:, PACK * P : 2 * PACK * P], odd[1][:])
         quantize(q_codes[0], q_scales[0], qb[0])
+        late_add(2, u[1][:], odd[2][:, :, 0:P])
         quantize(u_codes[0], u_scales[0], u[0])
-        add_pair(1, 1, even[:, :, groups[1]], odd[1][:, :, 0:P])
         quantize(q_codes[1], q_scales[1], qb[1])
-        add_pair(2, 1, even[:, :, groups[2]], odd[1][:, :, P:HALF])
+        late_add(3, u[2][:], odd[2][:, :, P:HALF])
         quantize(u_codes[1], u_scales[1], u[1])
         quantize(u_codes[2], u_scales[2], u[2])
 
@@ -146,7 +161,7 @@ def tile_attend_pre_rope_f_topk_kernel(tc, qT, kT, cT, wT, offs, offs2, out):
                     start=True,
                     stop=True,
                 )
-                copy = nc.vector.tensor_copy if (j, m) == (2, 1) else nc.scalar.copy
+                copy = nc.vector.tensor_copy if j > 0 and m == 1 else nc.scalar.copy
                 copy(res[g, m][:, lo : lo + widths[j]], acc[:])
                 if part.stop % HALF == 0:
                     nc.sync.dma_start(out=out_v[:, m, halves[g]], in_=res[g, m][:])

@@ -1,6 +1,7 @@
 from contextlib import ExitStack
 
 import concourse.mybir as mybir
+from concourse.masks import make_identity
 
 D, T, POS, N, NQ = 512, 2048, 1024, 512, 256
 FLOPS = 2 * D * N * NQ
@@ -50,17 +51,22 @@ def tile_attend_pre_rope_f_topk_kernel(tc, qT, kT, cT, wT, offs, offs2, out):
         nc.sync.dma_start(out=k3[:], in_=kv[:, 3 * T : 4 * T])
         nc.sync.dma_start(out=q_raw[:], in_=qT[0].rearrange("(p t) n -> p t n", t=PACK))
 
+        ident = pool.tile([P, P], F32, name="ident")
+        make_identity(nc, ident[:])
+
         kg01 = pool.tile([P, 2, N], F32, name="kg01")
         kg2 = pool.tile([P, N], F32, name="kg2")
         sin0 = pool.tile([P, N], F32, name="sin0")
         cos0_listed = [pool.tile([P, HALF], F32, name="cos0_listed%d" % g) for g in range(2)]
         by_sin = pool.tile([P, 2, N], F32, name="by_sin")
         by_cos = [pool.tile([P, 2, HALF], F32, name="by_cos%d" % g) for g in range(2)]
-        late = (slice(0, P), slice(P, HALF), slice(HALF, N))
-        kg3 = {i: pool.tile([P, late[i].stop - late[i].start], F32, name="kg3%d" % i) for i in (1, 2)}
+        kg3 = [pool.tile([P, P], F32, name="kg3%d" % j) for j in range(3)]
         factors = pool.tile([P, 3, N], F32, name="factors")
-        even = pool.tile([P, 2, N], F32, name="even")
-        odd = [pool.tile([P, 2, part.stop - part.start], F32, name="odd%d" % i) for i, part in enumerate(late)]
+        even = [pool.tile([P, 2, HALF], F32, name="even%d" % g) for g in range(2)]
+        odd = [pool.tile([P, 2, P], F32, name="odd%d" % j) for j in range(CHUNKS)]
+        sums = psum.tile([P, 2, P], F32, name="sums", tag="sums")
+        back = psum.tile([P, P], F32, name="back", tag="back")
+        turned = pool.tile([P, P], F32, name="turned")
         groups = (slice(0, HALF), slice(HALF, HALF + P), slice(HALF + P, N))
         widths = [part.stop - part.start for part in groups]
         u = [pool.tile([P, w * PACK], BF16, name="u%d" % j, align_bytes=64) for j, w in enumerate(widths)]
@@ -111,47 +117,63 @@ def tile_attend_pre_rope_f_topk_kernel(tc, qT, kT, cT, wT, offs, offs2, out):
         for j, part in enumerate(groups):
             lo = part.start % HALF
             add_pair(u[j][:], 0, by_cos[part.start // HALF][:, :, lo : lo + widths[j]], by_sin[:, :, part])
-        scalar_gather(kg2[:], k2[:], tok, every)
-        nc.vector.tensor_tensor(even[:, 1, :], kg2[:], factors[:, 2, :], MULT)
-        for part in halves:
-            scalar_gather(factors[:, 1, part], cos[1][:], pos, part)
-            nc.vector.tensor_tensor(even[:, 0, part], kg2[:, part], factors[:, 1, part], MULT)
+        for g in (1, 0):
+            scalar_gather(kg2[:, halves[g]], k2[:], tok, halves[g])
+            nc.vector.tensor_tensor(even[g][:, 1, :], kg2[:, halves[g]], factors[:, 2, halves[g]], MULT)
+        for g in (1, 0):
+            scalar_gather(factors[:, 1, halves[g]], cos[1][:], pos, halves[g])
+            nc.vector.tensor_tensor(even[g][:, 0, :], kg2[:, halves[g]], factors[:, 1, halves[g]], MULT)
 
-        for i in (1, 2):
-            scalar_gather(kg3[i][:], k3[:], tok, late[i])
-        for m in range(2):
+        def turn(e, src, start, stop):
+            nc.tensor.matmul(sums[:, e, :], src, ident[:], start=start, stop=stop, is_transpose=True)
+
+        for e in (1, 0):
+            turn(e, even[1][:, e, P:HALF], e == 1, False)
+
+        def cast_queries(m):
             nc.scalar.copy(
                 qb[m][:].rearrange("p (c i t) -> p c t i", i=4, t=PACK),
                 q_raw[:, :, slots(m)].rearrange("p t (c i) -> p c t i", i=4),
             )
 
-        def late_product(i):
-            width = late[i].stop - late[i].start
-            nc.vector.tensor_tensor(odd[i][:], twice(kg3[i][:], width), factors[:, 0:2, late[i]], MULT)
+        def late_product(j):
+            nc.vector.tensor_tensor(odd[j][:], twice(kg3[j][:], P), factors[:, 0:2, slots(j)], MULT)
 
-        def late_add(j, dst, src):
-            add_pair(dst, 1, even[:, :, slots(j)], src)
+        def late_add(j, dst):
+            add_pair(dst, 1, even[j // 2][:, :, slots(j % 2)], odd[j][:])
 
+        for j in range(3):
+            scalar_gather(kg3[j][:], k3[:], tok, slots(j))
         for e in range(2):
-            nc.vector.tensor_tensor(odd[0][:, e, :], listed(k3[:], tok, late[0]), factors[:, e, late[0]], MULT)
+            nc.vector.tensor_tensor(odd[3][:, e, :], listed(k3[:], tok, slots(3)), factors[:, e, slots(3)], MULT)
+            turn(e, odd[3][:, e, :], False, e == 1)
+        nc.scalar.copy(
+            turned[:].bitcast(BF16).rearrange("s (c i e) -> s c e i", i=4, e=2),
+            sums[:].rearrange("s e (c i) -> s c e i", i=4),
+        )
+        cast_queries(0)
+        cast_queries(1)
+        nc.tensor.transpose(back[:], turned[:], ident[:])
+        nc.scalar.copy(u[2][:].bitcast(F32).rearrange("p (n h) -> p n h", h=2)[:, :, 1], back[:])
+        late_product(0)
         late_product(1)
-        late_add(0, u[0][:, 0 : PACK * P], odd[0][:])
+        late_add(0, u[0][:, 0 : PACK * P])
         late_product(2)
-        late_add(1, u[0][:, PACK * P : 2 * PACK * P], odd[1][:])
+        late_add(1, u[0][:, PACK * P : 2 * PACK * P])
         quantize(q_codes[0], q_scales[0], qb[0])
-        late_add(2, u[1][:], odd[2][:, :, 0:P])
         quantize(u_codes[0], u_scales[0], u[0])
         quantize(q_codes[1], q_scales[1], qb[1])
-        late_add(3, u[2][:], odd[2][:, :, P:HALF])
-        quantize(u_codes[1], u_scales[1], u[1])
+        late_add(2, u[1][:])
         quantize(u_codes[2], u_scales[2], u[2])
+        quantize(u_codes[1], u_scales[1], u[1])
 
         res = {(g, m): pool.tile([P, HALF], F32, name="res%d%d" % (g, m)) for g in range(2) for m in range(2)}
-        for j, part in enumerate(groups):
+        for j in (0, 2, 1):
+            part = groups[j]
             g = part.start // HALF
             lo = part.start % HALF
             for m in range(2):
-                acc = psum.tile([P, widths[j]], F32, name="acc%d%d" % (j, m))
+                acc = psum.tile([P, widths[j]], F32, name="acc%d%d" % (j, m), tag="sums" if (j, m) == (0, 0) else "acc%d%d" % (j, m))
                 nc.tensor.matmul_mx(
                     out=acc[:],
                     lhsT=q_codes[m][:].bitcast(FP8X4),
@@ -163,5 +185,5 @@ def tile_attend_pre_rope_f_topk_kernel(tc, qT, kT, cT, wT, offs, offs2, out):
                 )
                 copy = nc.vector.tensor_copy if j > 0 and m == 1 else nc.scalar.copy
                 copy(res[g, m][:, lo : lo + widths[j]], acc[:])
-                if part.stop % HALF == 0:
+                if j < 2:
                     nc.sync.dma_start(out=out_v[:, m, halves[g]], in_=res[g, m][:])

@@ -27,6 +27,7 @@ def tile_attend_pre_rope_f_topk_kernel(tc, qT, kT, cT, wT, offs, offs2, out):
     nc = tc.nc
     with ExitStack() as ctx:
         pool = ctx.enter_context(tc.tile_pool(name="held", bufs=1))
+        reused = ctx.enter_context(tc.tile_pool(name="reused", bufs=1))
         psum = ctx.enter_context(tc.psum_pool(name="psum", bufs=1))
 
         tok = pool.tile([P, N // 16], U16, name="tok")
@@ -55,18 +56,19 @@ def tile_attend_pre_rope_f_topk_kernel(tc, qT, kT, cT, wT, offs, offs2, out):
         make_identity(nc, ident[:])
 
         kg01 = pool.tile([P, 2, N], F32, name="kg01")
-        kg2 = pool.tile([P, N], F32, name="kg2")
+        kg2 = [reused.tile([P, HALF], F32, name="kg2%d" % g, offset=4 * HALF * g) for g in range(2)]
         sin0 = pool.tile([P, N], F32, name="sin0")
         cos0_listed = [pool.tile([P, HALF], F32, name="cos0_listed%d" % g) for g in range(2)]
         by_sin = pool.tile([P, 2, N], F32, name="by_sin")
         by_cos = [pool.tile([P, 2, HALF], F32, name="by_cos%d" % g) for g in range(2)]
         kg3 = [pool.tile([P, P], F32, name="kg3%d" % j) for j in range(3)]
-        factors = pool.tile([P, 3, N], F32, name="factors")
+        factors = pool.tile([P, 2, N], F32, name="factors")
+        sin1 = pool.tile([P, N], F32, name="sin1")
         even = [pool.tile([P, 2, HALF], F32, name="even%d" % g) for g in range(2)]
-        odd = [pool.tile([P, 2, P], F32, name="odd%d" % j) for j in range(CHUNKS)]
+        odd = [reused.tile([P, 2, P], F32, name="odd%d" % j, offset=4 * (N + 2 * P * j)) for j in range(CHUNKS)]
         sums = psum.tile([P, 2, P], F32, name="sums", tag="sums")
-        back = psum.tile([P, P], F32, name="back", tag="back")
-        turned = pool.tile([P, P], F32, name="turned")
+        sums0 = psum.tile([P, 2, P], F32, name="sums0", tag="sums0")
+        back = psum.tile([P, 2, P], F32, name="back", tag="back")
         groups = (slice(0, HALF), slice(HALF, HALF + P), slice(HALF + P, N))
         widths = [part.stop - part.start for part in groups]
         u = [pool.tile([P, w * PACK], BF16, name="u%d" % j, align_bytes=64) for j, w in enumerate(widths)]
@@ -100,35 +102,47 @@ def tile_attend_pre_rope_f_topk_kernel(tc, qT, kT, cT, wT, offs, offs2, out):
         def quantize(codes, scales, src):
             nc.vector.quantize_mx(out=codes[:].bitcast(FP8X4), scales=scales[:], in_=src[:])
 
+        def turn(dst, src, start, stop):
+            nc.tensor.matmul(dst, src, ident[:], start=start, stop=stop, is_transpose=True)
+
+        def round_turned(dst, src):
+            nc.scalar.copy(
+                dst.bitcast(BF16).rearrange("s (c i e) -> s c e i", i=4, e=2),
+                src[:].rearrange("s e (c i) -> s c e i", i=4),
+            )
+
         every = slice(0, N)
         halves = (slice(0, HALF), slice(HALF, N))
 
-        nc.vector.tensor_copy(factors[:, 2, :], listed(sin[:, POS : 2 * POS], pos, every))
-        nc.scalar.activation(factors[:, 0, :], factors[:, 2, :], COPY, scale=-1.0)
+        nc.vector.tensor_copy(sin1[:], listed(sin[:, POS : 2 * POS], pos, every))
+        nc.scalar.activation(factors[:, 0, :], sin1[:], COPY, scale=-1.0)
         nc.vector.tensor_copy(sin0[:], listed(sin[:, 0:POS], pos, every))
         nc.vector.tensor_copy(kg01[:, 0, :], listed(k01[:, 0:T], tok, every))
         scalar_gather(kg01[:, 1, :], k01[:, T : 2 * T], tok, every)
-        for g, part in enumerate(halves):
-            scalar_gather(cos0_listed[g][:], cos[0][:], pos, part)
+        for g in (1, 0):
+            scalar_gather(cos0_listed[g][:], cos[0][:], pos, halves[g])
         nc.vector.scalar_tensor_tensor(by_sin[:, 0, :], kg01[:, 1, :], -1.0, sin0[:], MULT, MULT)
         nc.vector.tensor_tensor(by_sin[:, 1, :], kg01[:, 0, :], sin0[:], MULT)
-        for g, part in enumerate(halves):
-            nc.vector.tensor_tensor(by_cos[g][:], kg01[:, :, part], twice(cos0_listed[g][:], HALF), MULT)
-        for j, part in enumerate(groups):
-            lo = part.start % HALF
-            add_pair(u[j][:], 0, by_cos[part.start // HALF][:, :, lo : lo + widths[j]], by_sin[:, :, part])
         for g in (1, 0):
-            scalar_gather(kg2[:, halves[g]], k2[:], tok, halves[g])
-            nc.vector.tensor_tensor(even[g][:, 1, :], kg2[:, halves[g]], factors[:, 2, halves[g]], MULT)
+            nc.vector.tensor_tensor(by_cos[g][:], kg01[:, :, halves[g]], twice(cos0_listed[g][:], HALF), MULT)
+        for e in range(2):
+            turn(sums0[:, e, :], by_sin[:, e, groups[2]], e == 0, False)
+        for e in range(2):
+            turn(sums0[:, e, :], by_cos[1][:, e, P:HALF], False, e == 1)
+        for j in (1, 0):
+            add_pair(u[j][:], 0, by_cos[j][:, :, 0 : widths[j]], by_sin[:, :, groups[j]])
+        for g in (1, 0):
+            scalar_gather(kg2[g][:], k2[:], tok, halves[g])
+            nc.vector.tensor_tensor(even[g][:, 1, :], kg2[g][:], sin1[:, halves[g]], MULT)
         for g in (1, 0):
             scalar_gather(factors[:, 1, halves[g]], cos[1][:], pos, halves[g])
-            nc.vector.tensor_tensor(even[g][:, 0, :], kg2[:, halves[g]], factors[:, 1, halves[g]], MULT)
-
-        def turn(e, src, start, stop):
-            nc.tensor.matmul(sums[:, e, :], src, ident[:], start=start, stop=stop, is_transpose=True)
+            nc.vector.tensor_tensor(even[g][:, 0, :], kg2[g][:], factors[:, 1, halves[g]], MULT)
 
         for e in (1, 0):
-            turn(e, even[1][:, e, P:HALF], e == 1, False)
+            turn(sums[:, e, :], even[1][:, e, P:HALF], e == 1, False)
+        turned0 = reused.tile([P, P], F32, name="turned0", offset=4 * HALF)
+        round_turned(turned0[:], sums0)
+        nc.tensor.transpose(back[:, 0, :], turned0[:], ident[:])
 
         def cast_queries(m):
             nc.scalar.copy(
@@ -146,34 +160,32 @@ def tile_attend_pre_rope_f_topk_kernel(tc, qT, kT, cT, wT, offs, offs2, out):
             scalar_gather(kg3[j][:], k3[:], tok, slots(j))
         for e in range(2):
             nc.vector.tensor_tensor(odd[3][:, e, :], listed(k3[:], tok, slots(3)), factors[:, e, slots(3)], MULT)
-            turn(e, odd[3][:, e, :], False, e == 1)
-        nc.scalar.copy(
-            turned[:].bitcast(BF16).rearrange("s (c i e) -> s c e i", i=4, e=2),
-            sums[:].rearrange("s e (c i) -> s c e i", i=4),
-        )
+            turn(sums[:, e, :], odd[3][:, e, :], False, e == 1)
         cast_queries(0)
-        cast_queries(1)
-        nc.tensor.transpose(back[:], turned[:], ident[:])
-        nc.scalar.copy(u[2][:].bitcast(F32).rearrange("p (n h) -> p n h", h=2)[:, :, 1], back[:])
         late_product(0)
         late_product(1)
         late_add(0, u[0][:, 0 : PACK * P])
+        turned = reused.tile([P, P], F32, name="turned", offset=4 * N)
+        round_turned(turned[:], sums)
+        nc.tensor.transpose(back[:, 1, :], turned[:], ident[:])
+        cast_queries(1)
+        nc.scalar.copy(u[2][:].bitcast(F32).rearrange("p (n h) -> p n h", h=2), back[:].rearrange("p h n -> p n h"))
         late_product(2)
         late_add(1, u[0][:, PACK * P : 2 * PACK * P])
         quantize(q_codes[0], q_scales[0], qb[0])
         quantize(u_codes[0], u_scales[0], u[0])
-        quantize(q_codes[1], q_scales[1], qb[1])
         late_add(2, u[1][:])
-        quantize(u_codes[2], u_scales[2], u[2])
+        quantize(q_codes[1], q_scales[1], qb[1])
         quantize(u_codes[1], u_scales[1], u[1])
+        quantize(u_codes[2], u_scales[2], u[2])
 
         res = {(g, m): pool.tile([P, HALF], F32, name="res%d%d" % (g, m)) for g in range(2) for m in range(2)}
-        for j in (0, 2, 1):
+        for j in (0, 1, 2):
             part = groups[j]
             g = part.start // HALF
             lo = part.start % HALF
             for m in range(2):
-                acc = psum.tile([P, widths[j]], F32, name="acc%d%d" % (j, m), tag="sums" if (j, m) == (0, 0) else "acc%d%d" % (j, m))
+                acc = psum.tile([P, widths[j]], F32, name="acc%d%d" % (j, m), tag={(0, 0): "sums", (2, 1): "sums0"}.get((j, m), "acc%d%d" % (j, m)))
                 nc.tensor.matmul_mx(
                     out=acc[:],
                     lhsT=q_codes[m][:].bitcast(FP8X4),
@@ -183,7 +195,7 @@ def tile_attend_pre_rope_f_topk_kernel(tc, qT, kT, cT, wT, offs, offs2, out):
                     start=True,
                     stop=True,
                 )
-                copy = nc.vector.tensor_copy if j > 0 and m == 1 else nc.scalar.copy
+                copy = (nc.scalar.copy, nc.vector.tensor_copy)[m]
                 copy(res[g, m][:, lo : lo + widths[j]], acc[:])
-                if j < 2:
+                if j != 1:
                     nc.sync.dma_start(out=out_v[:, m, halves[g]], in_=res[g, m][:])

@@ -42,7 +42,7 @@ def tile_attend_pre_rope_f_topk_kernel(tc, qT, kT, cT, wT, offs, offs2, out):
         cv = cT.rearrange("(p t) n -> p t n", t=PACK)
         wv = wT.rearrange("(p t) n -> p (t n)", t=PACK)
 
-        nc.sync.dma_start(out=sin[:], in_=wv[:, POS : 3 * POS])
+        nc.scalar.dma_start(out=sin[:], in_=wv[:, POS : 3 * POS])
         nc.sync.dma_start(pos[:], offs2)
         nc.sync.dma_start(tok[:], offs)
         nc.sync.dma_start(out=k01[:], in_=kv[:, 0 : 2 * T])

@@ -180,22 +180,22 @@ def tile_attend_pre_rope_f_topk_kernel(tc, qT, kT, cT, wT, offs, offs2, out):
         quantize(u_codes[2], u_scales[2], u[2])
 
         res = {(g, m): pool.tile([P, HALF], F32, name="res%d%d" % (g, m)) for g in range(2) for m in range(2)}
-        for j in (0, 1, 2):
+        passes = [(0, m, a, a + P) for m in range(2) for a in (0, P)] + [(j, m, 0, P) for j in (1, 2) for m in range(2)]
+        for j, m, a, b in passes:
             part = groups[j]
             g = part.start // HALF
-            lo = part.start % HALF
-            for m in range(2):
-                acc = psum.tile([P, widths[j]], F32, name="acc%d%d" % (j, m), tag={(0, 0): "sums", (2, 1): "sums0"}.get((j, m), "acc%d%d" % (j, m)))
-                nc.tensor.matmul_mx(
-                    out=acc[:],
-                    lhsT=q_codes[m][:].bitcast(FP8X4),
-                    lhsT_scale=q_scales[m][:],
-                    rhs=u_codes[j][:].bitcast(FP8X4),
-                    rhs_scale=u_scales[j][:],
-                    start=True,
-                    stop=True,
-                )
-                copy = (nc.scalar.copy, nc.vector.tensor_copy)[m]
-                copy(res[g, m][:, lo : lo + widths[j]], acc[:])
-                if j != 1:
-                    nc.sync.dma_start(out=out_v[:, m, halves[g]], in_=res[g, m][:])
+            lo = part.start % HALF + a
+            acc = psum.tile([P, b - a], F32, name="acc%d%d%d" % (j, m, a), tag={(0, 0, 0): "sums", (0, 1, P): "back", (2, 1, 0): "sums0"}.get((j, m, a), "acc%d%d%d" % (j, m, a)))
+            nc.tensor.matmul_mx(
+                out=acc[:],
+                lhsT=q_codes[m][:].bitcast(FP8X4),
+                lhsT_scale=q_scales[m][:],
+                rhs=u_codes[j][:, a:b].bitcast(FP8X4),
+                rhs_scale=u_scales[j][:, a:b],
+                start=True,
+                stop=True,
+            )
+            copy = (nc.scalar.copy, nc.vector.tensor_copy)[m]
+            copy(res[g, m][:, lo : lo + b - a], acc[:])
+            if lo + b - a == HALF:
+                nc.sync.dma_start(out=out_v[:, m, halves[g]], in_=res[g, m][:])

@@ -61,17 +61,19 @@ def tile_attend_pre_rope_f_topk_kernel(tc, qT, kT, cT, wT, offs, offs2, out):
         cos0_listed = [pool.tile([P, HALF], F32, name="cos0_listed%d" % g) for g in range(2)]
         by_sin = pool.tile([P, 2, N], F32, name="by_sin")
         by_cos = [pool.tile([P, 2, HALF], F32, name="by_cos%d" % g) for g in range(2)]
-        kg3 = [pool.tile([P, P], F32, name="kg3%d" % j) for j in range(3)]
+        kg3 = [reused.tile([P, P], F32, name="kg3%d" % j, offset=4 * (N + P * j)) for j in range(3)]
+        words = pool.tile([P, 2, P], F32, name="words")
         factors = pool.tile([P, 2, N], F32, name="factors")
         sin1 = pool.tile([P, N], F32, name="sin1")
         even = [pool.tile([P, 2, HALF], F32, name="even%d" % g) for g in range(2)]
-        odd = [reused.tile([P, 2, P], F32, name="odd%d" % j, offset=4 * (N + 2 * P * j)) for j in range(CHUNKS)]
+        odd = [pool.tile([P, 2, P], F32, name="odd%d" % j) for j in range(CHUNKS)]
         sums = psum.tile([P, 2, P], F32, name="sums", tag="sums")
         sums0 = psum.tile([P, 2, P], F32, name="sums0", tag="sums0")
         back = psum.tile([P, 2, P], F32, name="back", tag="back")
         groups = (slice(0, HALF), slice(HALF, HALF + P), slice(HALF + P, N))
         widths = [part.stop - part.start for part in groups]
-        u = [pool.tile([P, w * PACK], BF16, name="u%d" % j, align_bytes=64) for j, w in enumerate(widths)]
+        u = [pool.tile([P, w * PACK], BF16, name="u%d" % j, align_bytes=64) for j, w in enumerate(widths[:2])]
+        u.append(reused.tile([P, P * PACK], BF16, name="u2", offset=4 * 2 * N, align_bytes=64))
         qb = [pool.tile([P, P * PACK], BF16, name="qb%d" % m, align_bytes=64) for m in range(2)]
         u_codes = [pool.tile([P, w], U32, name="u_codes%d" % j, align_bytes=64) for j, w in enumerate(widths)]
         u_scales = [pool.tile([P, w], U8, name="u_scales%d" % j, align_bytes=64) for j, w in enumerate(widths)]
@@ -96,6 +98,14 @@ def tile_attend_pre_rope_f_topk_kernel(tc, qT, kT, cT, wT, offs, offs2, out):
                 dst.rearrange("p (n t) -> p n t", t=PACK)[:, :, 2 * h : 2 * h + 2].rearrange("p (c i) e -> p c e i", i=2),
                 a.rearrange("p e (c i) -> p c e i", i=2),
                 b.rearrange("p e (c i) -> p c e i", i=2),
+                ADD,
+            )
+
+        def add_words(h, a, b):
+            nc.vector.tensor_tensor(
+                words[:, h, :].bitcast(BF16).rearrange("p (c i e) -> p c e i", i=4, e=2),
+                a.rearrange("p e (c i) -> p c e i", i=4),
+                b.rearrange("p e (c i) -> p c e i", i=4),
                 ADD,
             )
 
@@ -129,8 +139,8 @@ def tile_attend_pre_rope_f_topk_kernel(tc, qT, kT, cT, wT, offs, offs2, out):
             turn(sums0[:, e, :], by_sin[:, e, groups[2]], e == 0, False)
         for e in range(2):
             turn(sums0[:, e, :], by_cos[1][:, e, P:HALF], False, e == 1)
-        for j in (1, 0):
-            add_pair(u[j][:], 0, by_cos[j][:, :, 0 : widths[j]], by_sin[:, :, groups[j]])
+        add_words(0, by_cos[1][:, :, 0:P], by_sin[:, :, groups[1]])
+        add_pair(u[0][:], 0, by_cos[0][:], by_sin[:, :, groups[0]])
         for g in (1, 0):
             scalar_gather(kg2[g][:], k2[:], tok, halves[g])
             nc.vector.tensor_tensor(even[g][:, 1, :], kg2[g][:], sin1[:, halves[g]], MULT)
@@ -165,21 +175,23 @@ def tile_attend_pre_rope_f_topk_kernel(tc, qT, kT, cT, wT, offs, offs2, out):
         late_product(0)
         late_product(1)
         late_add(0, u[0][:, 0 : PACK * P])
-        turned = reused.tile([P, P], F32, name="turned", offset=4 * N)
+        turned = reused.tile([P, P], F32, name="turned", offset=4 * (N + P))
         round_turned(turned[:], sums)
         nc.tensor.transpose(back[:, 1, :], turned[:], ident[:])
         cast_queries(1)
-        nc.scalar.copy(u[2][:].bitcast(F32).rearrange("p (n h) -> p n h", h=2), back[:].rearrange("p h n -> p n h"))
         late_product(2)
         late_add(1, u[0][:, PACK * P : 2 * PACK * P])
+        add_words(1, even[1][:, :, 0:P], odd[2][:])
+        for j, pairs in ((1, words), (2, back)):
+            nc.scalar.copy(u[j][:].bitcast(F32).rearrange("p (n h) -> p n h", h=2), pairs[:].rearrange("p h n -> p n h"))
         quantize(q_codes[0], q_scales[0], qb[0])
         quantize(u_codes[0], u_scales[0], u[0])
-        late_add(2, u[1][:])
         quantize(q_codes[1], q_scales[1], qb[1])
         quantize(u_codes[1], u_scales[1], u[1])
         quantize(u_codes[2], u_scales[2], u[2])
 
-        res = {(g, m): pool.tile([P, HALF], F32, name="res%d%d" % (g, m)) for g in range(2) for m in range(2)}
+        res = {gm: pool.tile([P, HALF], F32, name="res%d%d" % gm) for gm in ((0, 0), (1, 0), (1, 1))}
+        res[0, 1] = reused.tile([P, HALF], F32, name="res01", offset=4 * 2 * N, align_bytes=64)
         passes = [(0, m, a, a + P) for m in range(2) for a in (0, P)] + [(j, m, 0, P) for j in (1, 2) for m in range(2)]
         for j, m, a, b in passes:
             part = groups[j]
@@ -195,7 +207,7 @@ def tile_attend_pre_rope_f_topk_kernel(tc, qT, kT, cT, wT, offs, offs2, out):
                 start=True,
                 stop=True,
             )
-            copy = (nc.scalar.copy, nc.vector.tensor_copy)[m]
+            copy = nc.vector.tensor_copy if m == 1 and (j, a) != (0, 0) else nc.scalar.copy
             copy(res[g, m][:, lo : lo + b - a], acc[:])
             if lo + b - a == HALF:
                 nc.sync.dma_start(out=out_v[:, m, halves[g]], in_=res[g, m][:])

from contextlib import ExitStack

import concourse.mybir as mybir
from concourse.masks import make_identity

D, T, POS, N, NQ = 512, 2048, 1024, 512, 256
FLOPS = 2 * D * N * NQ
BYTES = 4 * (D * NQ + D * T + D * POS + NQ * N) + 2 * 2 * 128 * (N // 16)

F32 = mybir.dt.float32
BF16 = mybir.dt.bfloat16
U32 = mybir.dt.uint32
U16 = mybir.dt.uint16
U8 = mybir.dt.uint8
FP8X4 = mybir.dt.float8_e4m3fn_x4
MULT = mybir.AluOpType.mult
ADD = mybir.AluOpType.add
COPY = mybir.ActivationFunctionType.Copy

P = 128
PACK = 4
CHUNKS = N // P
HALF = N // 2


def tile_attend_pre_rope_f_topk_kernel(tc, qT, kT, cT, wT, offs, offs2, out):
    nc = tc.nc
    with ExitStack() as ctx:
        pool = ctx.enter_context(tc.tile_pool(name="held", bufs=1))
        reused = ctx.enter_context(tc.tile_pool(name="reused", bufs=1))
        psum = ctx.enter_context(tc.psum_pool(name="psum", bufs=1))

        tok = pool.tile([P, N // 16], U16, name="tok")
        pos = pool.tile([P, N // 16], U16, name="pos")
        k01 = pool.tile([P, 2 * T], F32, name="k01")
        k2 = pool.tile([P, T], F32, name="k2")
        k3 = pool.tile([P, T], F32, name="k3")
        cos = [pool.tile([P, POS], F32, name="cos%d" % h) for h in range(2)]
        sin = pool.tile([P, 2 * POS], F32, name="sin")
        q_raw = pool.tile([P, PACK, NQ], F32, name="q_raw")
        kv = kT.rearrange("(p t) n -> p (t n)", t=PACK)
        cv = cT.rearrange("(p t) n -> p t n", t=PACK)
        wv = wT.rearrange("(p t) n -> p (t n)", t=PACK)

        nc.scalar.dma_start(out=sin[:], in_=wv[:, POS : 3 * POS])
        nc.sync.dma_start(pos[:], offs2)
        nc.sync.dma_start(tok[:], offs)
        nc.sync.dma_start(out=k01[:], in_=kv[:, 0 : 2 * T])
        nc.sync.dma_start(out=cos[0][:], in_=cv[:, 0, :])
        nc.sync.dma_start(out=k2[:], in_=kv[:, 2 * T : 3 * T])
        nc.sync.dma_start(out=cos[1][:], in_=cv[:, 2, :])
        nc.sync.dma_start(out=k3[:], in_=kv[:, 3 * T : 4 * T])
        nc.sync.dma_start(out=q_raw[:], in_=qT[0].rearrange("(p t) n -> p t n", t=PACK))

        ident = pool.tile([P, P], F32, name="ident")
        make_identity(nc, ident[:])

        kg01 = pool.tile([P, 2, N], F32, name="kg01")
        kg2 = [reused.tile([P, HALF], F32, name="kg2%d" % g, offset=4 * HALF * g) for g in range(2)]
        sin0 = pool.tile([P, N], F32, name="sin0")
        cos0_listed = [pool.tile([P, HALF], F32, name="cos0_listed%d" % g) for g in range(2)]
        by_sin = pool.tile([P, 2, N], F32, name="by_sin")
        by_cos = [pool.tile([P, 2, HALF], F32, name="by_cos%d" % g) for g in range(2)]
        kg3 = [reused.tile([P, P], F32, name="kg3%d" % j, offset=4 * (N + P * j)) for j in range(3)]
        words = pool.tile([P, 2, P], F32, name="words")
        factors = pool.tile([P, 2, N], F32, name="factors")
        sin1 = pool.tile([P, N], F32, name="sin1")
        even = [pool.tile([P, 2, HALF], F32, name="even%d" % g) for g in range(2)]
        odd = [pool.tile([P, 2, P], F32, name="odd%d" % j) for j in range(CHUNKS)]
        sums = psum.tile([P, 2, P], F32, name="sums", tag="sums")
        sums0 = psum.tile([P, 2, P], F32, name="sums0", tag="sums0")
        back = psum.tile([P, 2, P], F32, name="back", tag="back")
        groups = (slice(0, HALF), slice(HALF, HALF + P), slice(HALF + P, N))
        widths = [part.stop - part.start for part in groups]
        u = [pool.tile([P, w * PACK], BF16, name="u%d" % j, align_bytes=64) for j, w in enumerate(widths[:2])]
        u.append(reused.tile([P, P * PACK], BF16, name="u2", offset=4 * 2 * N, align_bytes=64))
        qb = [pool.tile([P, P * PACK], BF16, name="qb%d" % m, align_bytes=64) for m in range(2)]
        u_codes = [pool.tile([P, w], U32, name="u_codes%d" % j, align_bytes=64) for j, w in enumerate(widths)]
        u_scales = [pool.tile([P, w], U8, name="u_scales%d" % j, align_bytes=64) for j, w in enumerate(widths)]
        q_codes = [pool.tile([P, P], U32, name="q_codes%d" % m, align_bytes=64) for m in range(2)]
        q_scales = [pool.tile([P, P], U8, name="q_scales%d" % m, align_bytes=64) for m in range(2)]
        out_v = out[0].rearrange("(m p) n -> p m n", p=P)

        def slots(j):
            return slice(j * P, (j + 1) * P)

        def listed(window, offsets, part):
            return window.indirect(offsets[:, part.start // 16 : part.stop // 16])

        def scalar_gather(dst, window, offsets, part):
            nc.scalar.activation(dst, listed(window, offsets, part), COPY)

        def twice(src, width):
            return src.unsqueeze(1).to_broadcast([P, 2, width])

        def add_pair(dst, h, a, b):
            nc.vector.tensor_tensor(
                dst.rearrange("p (n t) -> p n t", t=PACK)[:, :, 2 * h : 2 * h + 2].rearrange("p (c i) e -> p c e i", i=2),
                a.rearrange("p e (c i) -> p c e i", i=2),
                b.rearrange("p e (c i) -> p c e i", i=2),
                ADD,
            )

        def add_words(h, a, b):
            nc.vector.tensor_tensor(
                words[:, h, :].bitcast(BF16).rearrange("p (c i e) -> p c e i", i=4, e=2),
                a.rearrange("p e (c i) -> p c e i", i=4),
                b.rearrange("p e (c i) -> p c e i", i=4),
                ADD,
            )

        def quantize(codes, scales, src):
            nc.vector.quantize_mx(out=codes[:].bitcast(FP8X4), scales=scales[:], in_=src[:])

        def turn(dst, src, start, stop):
            nc.tensor.matmul(dst, src, ident[:], start=start, stop=stop, is_transpose=True)

        def round_turned(dst, src):
            nc.scalar.copy(
                dst.bitcast(BF16).rearrange("s (c i e) -> s c e i", i=4, e=2),
                src[:].rearrange("s e (c i) -> s c e i", i=4),
            )

        every = slice(0, N)
        halves = (slice(0, HALF), slice(HALF, N))

        nc.vector.tensor_copy(sin1[:], listed(sin[:, POS : 2 * POS], pos, every))
        nc.scalar.activation(factors[:, 0, :], sin1[:], COPY, scale=-1.0)
        nc.vector.tensor_copy(sin0[:], listed(sin[:, 0:POS], pos, every))
        nc.vector.tensor_copy(kg01[:, 0, :], listed(k01[:, 0:T], tok, every))
        scalar_gather(kg01[:, 1, :], k01[:, T : 2 * T], tok, every)
        for g in (1, 0):
            scalar_gather(cos0_listed[g][:], cos[0][:], pos, halves[g])
        nc.vector.scalar_tensor_tensor(by_sin[:, 0, :], kg01[:, 1, :], -1.0, sin0[:], MULT, MULT)
        nc.vector.tensor_tensor(by_sin[:, 1, :], kg01[:, 0, :], sin0[:], MULT)
        for g in (1, 0):
            nc.vector.tensor_tensor(by_cos[g][:], kg01[:, :, halves[g]], twice(cos0_listed[g][:], HALF), MULT)
        for e in range(2):
            turn(sums0[:, e, :], by_sin[:, e, groups[2]], e == 0, False)
        for e in range(2):
            turn(sums0[:, e, :], by_cos[1][:, e, P:HALF], False, e == 1)
        add_words(0, by_cos[1][:, :, 0:P], by_sin[:, :, groups[1]])
        add_pair(u[0][:], 0, by_cos[0][:], by_sin[:, :, groups[0]])
        for g in (1, 0):
            scalar_gather(kg2[g][:], k2[:], tok, halves[g])
            nc.vector.tensor_tensor(even[g][:, 1, :], kg2[g][:], sin1[:, halves[g]], MULT)
        for g in (1, 0):
            scalar_gather(factors[:, 1, halves[g]], cos[1][:], pos, halves[g])
            nc.vector.tensor_tensor(even[g][:, 0, :], kg2[g][:], factors[:, 1, halves[g]], MULT)

        for e in (1, 0):
            turn(sums[:, e, :], even[1][:, e, P:HALF], e == 1, False)
        turned0 = reused.tile([P, P], F32, name="turned0", offset=4 * HALF)
        round_turned(turned0[:], sums0)
        nc.tensor.transpose(back[:, 0, :], turned0[:], ident[:])

        def cast_queries(m):
            nc.scalar.copy(
                qb[m][:].rearrange("p (c i t) -> p c t i", i=4, t=PACK),
                q_raw[:, :, slots(m)].rearrange("p t (c i) -> p c t i", i=4),
            )

        def late_product(j):
            nc.vector.tensor_tensor(odd[j][:], twice(kg3[j][:], P), factors[:, 0:2, slots(j)], MULT)

        def late_add(j, dst):
            add_pair(dst, 1, even[j // 2][:, :, slots(j % 2)], odd[j][:])

        for j in range(3):
            scalar_gather(kg3[j][:], k3[:], tok, slots(j))
        for e in range(2):
            nc.vector.tensor_tensor(odd[3][:, e, :], listed(k3[:], tok, slots(3)), factors[:, e, slots(3)], MULT)
            turn(sums[:, e, :], odd[3][:, e, :], False, e == 1)
        cast_queries(0)
        late_product(0)
        late_product(1)
        late_add(0, u[0][:, 0 : PACK * P])
        turned = reused.tile([P, P], F32, name="turned", offset=4 * (N + P))
        round_turned(turned[:], sums)
        nc.tensor.transpose(back[:, 1, :], turned[:], ident[:])
        cast_queries(1)
        late_product(2)
        late_add(1, u[0][:, PACK * P : 2 * PACK * P])
        add_words(1, even[1][:, :, 0:P], odd[2][:])
        for j, pairs in ((1, words), (2, back)):
            nc.scalar.copy(u[j][:].bitcast(F32).rearrange("p (n h) -> p n h", h=2), pairs[:].rearrange("p h n -> p n h"))
        quantize(q_codes[0], q_scales[0], qb[0])
        quantize(u_codes[0], u_scales[0], u[0])
        quantize(q_codes[1], q_scales[1], qb[1])
        quantize(u_codes[1], u_scales[1], u[1])
        quantize(u_codes[2], u_scales[2], u[2])

        res = {gm: pool.tile([P, HALF], F32, name="res%d%d" % gm) for gm in ((0, 0), (1, 0), (1, 1))}
        res[0, 1] = reused.tile([P, HALF], F32, name="res01", offset=4 * 2 * N, align_bytes=64)
        passes = [(0, m, a, a + P) for m in range(2) for a in (0, P)] + [(j, m, 0, P) for j in (1, 2) for m in range(2)]
        for j, m, a, b in passes:
            part = groups[j]
            g = part.start // HALF
            lo = part.start % HALF + a
            acc = psum.tile([P, b - a], F32, name="acc%d%d%d" % (j, m, a), tag={(0, 0, 0): "sums", (0, 1, P): "back", (2, 1, 0): "sums0"}.get((j, m, a), "acc%d%d%d" % (j, m, a)))
            nc.tensor.matmul_mx(
                out=acc[:],
                lhsT=q_codes[m][:].bitcast(FP8X4),
                lhsT_scale=q_scales[m][:],
                rhs=u_codes[j][:, a:b].bitcast(FP8X4),
                rhs_scale=u_scales[j][:, a:b],
                start=True,
                stop=True,
            )
            copy = nc.vector.tensor_copy if m == 1 and (j, a) != (0, 0) else nc.scalar.copy
            copy(res[g, m][:, lo : lo + b - a], acc[:])
            if lo + b - a == HALF:
                nc.sync.dma_start(out=out_v[:, m, halves[g]], in_=res[g, m][:])
